import numpy as np, ml_dtypes
CORES = [40,41,42,43,44,45,46,47]
N = 8
BF = ml_dtypes.bfloat16
W, B, RO, NEED = 2048, 256, 3, 8
def spot(o, u, t):
    return (((o * (2 * u + 1)) >> 5) + o + 77 * t) & (W - 1)
def base(rng):
    amp = rng.integers(32, 256, (N, 8, 1, W))
    return {"hue": (rng.random((N, 8, 16, W)) * (amp + 1)).astype(np.int64), "own": rng.integers(0, W, (N, 8, 16, B)), "nb": rng.integers(0, B, (N, 8, 16, B)),
            "tau": rng.integers(0, B, (N, 8, B)), "prev": rng.integers(0, B, (N, 8, B)), "foe": rng.integers(0, B, (N, 8, B)),
            "tas": rng.integers(0, 1024, (N, 8, B)), "wt": rng.integers(0, 256, (N, 8, 16, 1))}
def pack(d):
    out = {"hue": np.ascontiguousarray(d["hue"].reshape(N, 128, W)).astype(np.float32).astype(BF)}
    for k in ("own", "nb"): out[k] = np.ascontiguousarray(d[k].reshape(N, 128, B)).astype(np.int32)
    for k in ("tau", "prev", "foe", "tas"): out[k] = np.ascontiguousarray(d[k]).astype(np.int32)
    out["wt"] = np.ascontiguousarray(d["wt"].reshape(N, 128, 1)).astype(np.int32)
    return out
def setup_inputs(rng):
    return pack(base(rng))
def setup_inputs_ties(rng):
    d = base(rng)
    e = rng.choice(np.array([3.0, 6.0, 12.0]), (N, 8, 1, W)); m = rng.choice(np.array([1, 17, 85]), (N, 8, 1, 1)); m[0, 0] = 85; m[0, 1] = 1
    d["hue"] = np.minimum((4 * rng.random((N, 8, 16, W)) ** e).astype(np.int64), 3) * m
    pool = rng.integers(0, W, (N, 8, 24)); some = np.take_along_axis(pool, rng.integers(0, 24, (N, 8, 16 * B)), 2).reshape(N, 8, 16, B)
    d["own"][:, 1::2] = some[:, 1::2]; d["tas"][:, 1::2] = rng.choice(np.array([5, 512, 1000]), (N, 4, B))
    for a in (2, 5):
        d["own"][:, a, :, 1::2] = d["own"][:, a, :, 0::2]; d["tas"][:, a, 1::2] = d["tas"][:, a, 0::2]
    pool = rng.integers(0, B, (N, 8, 20)); few = np.take_along_axis(pool, rng.integers(0, 20, (N, 8, B)), 2)
    d["tau"][:, 3:] = few[:, 3:]
    return pack(d)
def setup_inputs_corners(rng):
    d = base(rng); b = np.arange(B)
    pats = np.stack([0 * b, 0 * b + B - 1, b, B - 1 - b, (b + 1) % B, (B - 1) * (b & 1), b >> 1, np.minimum(b + 1, B - 1)])
    ia = np.arange(8)[None, :] + np.arange(N)[:, None] + rng.integers(0, 8)
    d["tau"] = pats[ia & 7]; d["prev"] = pats[(ia + 3) & 7]; d["foe"] = pats[(ia + 5) & 7]; d["nb"] = pats[(ia[:, :, None] + np.arange(16)) & 7]
    d["tau"][0] = np.argsort(rng.random((8, B)), axis=1)
    d["tau"][0, :4] = np.stack([b, B - 1 - b, (b + 1) % B, (b + B - 1) % B])
    d["tau"][0, 6, 0] = d["tau"][0, 6, 1]
    d["hue"][0] = 128 + (d["hue"][0] >> 1); d["hue"][1] = d["hue"][1] & 1
    d["hue"][2] = 255; d["hue"][3, 7] = 255; d["tau"][2] = np.argsort(rng.random((8, B)), axis=1)
    kind = rng.integers(0, 5, (N, 8, 1, B)); one = d["own"][:, :, :1, :]; two = (W - 1) * rng.integers(0, 2, (N, 8, 16, B))
    o = d["own"]; o = np.where(kind == 0, 0, np.where(kind == 1, W - 1, np.where(kind == 2, one, np.where(kind == 3, two, o)))); d["own"] = o
    d["tas"] = np.where(rng.random((N, 8, B)) < 0.5, rng.choice(np.array([0, 1, 511, 512, 1023]), (N, 8, B)), d["tas"])
    d["wt"][:, 0] = 0; d["wt"][:, 7] = 255
    return pack(d)
def setup_inputs_close(rng):
    d = base(rng); b = np.arange(B); p = rng.permutation(N); s, m = int(p[0]), int(p[1]); o, u = d["own"], d["tas"]
    hn = (NEED - 1) // 2; nn = max(NEED, 17 - NEED); ca = int(spot(W - 1, 0, 0)); last = int(spot(W - 1, 1023, RO - 1))
    x = np.minimum(d["hue"], 253)
    x[:, 2:4, :, ca] = 254
    for a, lo in ((2, B - 1), (3, B // 2)):
        c = spot(o[:, a], u[:, a, None, :], 0); o[:, a] = np.where(c == ca, 0, o[:, a])
        o[:, a, 3, lo:] = W - 1; u[:, a, lo:] = 0
        d["tau"][:, a] = rng.integers(lo, B, (N, 1))
    x[:, 4, NEED - 1:] = 7; d["tau"][:, 4] = b; d["prev"][:, 4] = B - 1 - b
    for a, lo in ((5, 129), (6, 250)):
        x[:, a] = 0
        x[:, a, :hn] = lo + rng.integers(0, 4, (N, hn, W)); x[:, a, 8:8 + hn] = lo + rng.integers(0, 4, (N, hn, W))
        x[m, a] = rng.integers(0, 2, (16, W))
    x[:, 7, nn:, last] = 255; x[:, 7, nn:, W - 1] = 0
    o[:, 7] = np.where(np.argsort(rng.random((N, 16, B)), axis=1) < 10, W - 1, o[:, 7])
    x[s] = rng.integers(0, 16, (8, 16, W)); x[s, :, :nn] = 255
    u[s, 7] = 1023; d["wt"][s, 7] = 0; d["wt"][s, 7, 0, 0] = 255; d["wt"][s, 7, 1, 0] = 2
    d["hue"] = x
    return pack(d)
def setup_inputs_spread(rng):
    d = base(rng); lw = int(W).bit_length() - 1
    d["hue"] = np.minimum((np.exp2(8 * rng.random((N, 8, 1, W))) * rng.random((N, 8, 16, W))).astype(np.int64), 255)
    n = np.minimum(np.exp2(lw * rng.random((N, 8, 16, B))).astype(np.int64) - 1, W - 1)
    d["own"] = np.where(rng.random((N, 8, 16, B)) < 0.5, W - 1 - n, n)
    for k in ("tau", "prev", "foe"): d[k] = np.minimum((B * rng.random((N, 8, B)) ** rng.choice(np.array([1.0, 2.0, 4.0]), (N, 8, 1))).astype(np.int64), B - 1)
    d["nb"] = np.minimum((B * rng.random((N, 8, 16, B)) ** 2).astype(np.int64), B - 1)
    d["tas"] = np.minimum((1024 * rng.random((N, 8, B)) ** 3).astype(np.int64), 1023)
    d["wt"] = np.minimum(np.exp2(8 * rng.random((N, 8, 16, 1))).astype(np.int64), 255)
    return pack(d)
def setup_inputs_ends(rng):
    d = base(rng)
    def pick(hi, *s): return hi * rng.integers(0, 2, s)
    d["hue"] = pick(255, N, 8, 16, W); o = pick(W - 1, N, 8, 16, B); kind = rng.integers(0, 4, (N, 8, 1, B))
    o = np.where(kind == 0, 0, np.where(kind == 1, W - 1, o)); u = pick(1023, N, 8, B); ta = pick(B - 1, N, 8, B)
    for k in ("prev", "foe"): d[k] = pick(B - 1, N, 8, B)
    d["foe"] = np.where(rng.random((N, 8, B)) < 0.3, rng.integers(0, B, (N, 8, B)), d["foe"])
    d["nb"] = pick(B - 1, N, 8, 16, B); w = pick(255, N, 8, 16, 1); w[:, 7] = 255; w[:, 3] = 0
    ca, cb, cc, cd = spot(W - 1, 0, 0), spot(W - 1, 1023, 0), spot(W - 2, 1023, 0), spot(W - 2, 0, 0)
    cnt = np.array([NEED - 1, NEED, NEED - 1, NEED - 1, NEED, NEED - 1, NEED - 1, NEED - 1])
    d["hue"][..., 0] = 0; d["hue"][..., cd] = 0; d["hue"][..., cb] = 255; d["hue"][..., cc] = 255; d["hue"][:, :, 5, cc] = 254
    d["hue"][..., ca] = np.where(np.argsort(rng.random((N, 8, 16)), axis=2) < cnt[None, :, None], 255, 0)
    for v, p in ((0, (2, 14)), (B - 1, (3, 15))):
        o[..., v] = 0; o[:, :, 1, v] = W - 2; o[:, :, p[0], v] = W - 1; o[:, :, p[1], v] = W - 1; u[..., v] = 0
    ta[..., 0] = 0; ta[..., 1] = B - 1; o[..., 1] = 0; u[..., 1] = 1023
    o[..., B - 2] = W - 1; u[..., B - 2] = 1023
    ta[N - 1, 7] = 0; ta[N - 1, 7, B - 1] = B - 1; o[N - 1, 7, :, B - 1] = 0; u[N - 1, 7, B - 1] = 1023
    d["own"], d["tas"], d["tau"], d["wt"] = o, u, ta, w
    return pack(d)
def check_inputs(d):
    bad = []
    for k, hi in (("hue", 255), ("own", W - 1), ("nb", B - 1), ("tau", B - 1), ("prev", B - 1), ("foe", B - 1), ("tas", 1023), ("wt", 255)):
        v = np.asarray(d[k]).astype(np.float64)
        if not (np.min(v) >= 0 and np.max(v) <= hi): bad.append("range of " + k)
        elif np.any(v != np.floor(v)): bad.append("whole numbers of " + k)
    return bad
def look(x, names, u, t):
    c = spot(names, u[:, None, :], t).reshape(8, 1, 16 * B)
    return np.take_along_axis(x, c, 2).reshape(8, 16, 16, B)
def reference(hue, own, nb, tau, prev, foe, tas, wt):
    x = hue.astype(np.float32).astype(np.int64).reshape(N, 8, 16, W); o = own.astype(np.int64).reshape(N, 8, 16, B); nx = nb.astype(np.int64).reshape(N, 8, 16, B)
    ta, pr, fo, u = tau.astype(np.int64), prev.astype(np.int64), foe.astype(np.int64), tas.astype(np.int64)
    w = wt.astype(np.int64).reshape(N, 8, 16, 1); bird = np.arange(B)[None, :]; grp = np.arange(8)[:, None]
    for t in range(RO):
        dist = 1 + t % (N - 1); top, low, raids = [], [], []
        for r in range(N):
            v = look(x[r], o[r], u[r], t); m = np.max(v, axis=2); top.append(m)
            low.append(np.argmin(np.add.reduce((v == m[:, :, None, :]).astype(np.int64), axis=1), axis=1))
        for r in range(N):
            q = (r + dist) % N; ix = ta[r][:, None, :]
            y = look(x[q], np.take_along_axis(o[q], ix, 2), u[r], t)
            g = np.argmax(np.add.reduce(np.maximum(y - top[r][:, :, None, :], 0), axis=1), axis=1)
            ok = np.add.reduce((np.take_along_axis(top[q], ix, 2) > top[r]).astype(np.int64), axis=1) < NEED
            first = np.full((8, B), B, np.int64); np.minimum.at(first, (np.broadcast_to(grp, (8, B)), ta[r]), np.where(ok, bird, B))
            a, b = np.nonzero(ok & (np.take_along_axis(first, ta[r], 1) == bird))
            raids.append((r, q, a, b, ta[r][a, b], g[a, b], low[r][a, b]))
        no, nt, npr, nf = np.array(o), np.array(fo), np.array(pr), np.array(fo); stolen = np.zeros((N, 1, 1), np.int64)
        for r, q, a, b, v, g, j in raids:
            no[r, a, j, b] = o[q, a, g, v]; npr[r, a, b] = v; nt[r, a, b] = nx[q, a, g, v]
        for r, q, a, b, v, g, j in raids:
            no[q, a, g, v] = o[r, a, j, b]; nf[q, a, v] = b; nt[q, a, v] = pr[r, a, b]; stolen[q] = len(a)
        u = (np.add.reduce(w * np.stack(top), axis=2) + stolen) & 1023
        o, ta, pr, fo = no, nt, npr, nf
    return {"yo": o.reshape(N, 128, B).astype(np.float32), "yt": ta.astype(np.float32), "yp": pr.astype(np.float32), "yf": fo.astype(np.float32), "yu": u.astype(np.float32)}

@@ -1,0 +1,523 @@
+from concourse.mybir import AluOpType as A, ActivationFunctionType as F, AxisListType as AX
+
+N, RO, W = 8, 3, 2048
+BIG, TOP, RHO = float(2 ** 90), float(2 ** 74), 2.25
+HCH = [[("S", 0, 88), ("S", 88, 176), ("S", 176, 256)],
+       [("S", 0, 92), ("S", 92, 184), ("V", 184, 256)]]
+HORD = [(0, 1, 2), (2, 0, 1)]
+OFF = [(0, 12), (1, 12)]
+ENG = 16
+
+f32, bf, h16, i32, u16 = "float32", "bfloat16", "float16", "int32", "uint16"
+
+
+def sb(n, d, p=128):
+    return ("sbuf", [p, n], d)
+
+
+SCRATCH = {
+    "hue0": sb(W, bf), "hue1": sb(W, bf), "hue2": sb(W, bf),
+    "O": sb(256, i32), "X1": sb(256, i32), "PR": sb(256, i32), "SH": sb(256, i32), "PA": sb(256, i32), "SA": sb(256, i32),
+    "offH": sb(256, u16), "offA": sb(256, u16),
+    "xH": sb(4096, bf), "xP": sb(4096, bf), "ZH": sb(4096, bf), "xA": sb(4096, bf), "ZA": sb(4096, bf), "ZB": sb(1024, bf), "cg": sb(16, bf), "ONE16": sb(128, bf),
+    "Us": sb(768, bf), "Ul": sb(768, bf), "taus": sb(48, u16), "taul": sb(48, u16), "uEs": sb(1024, h16), "uEl": sb(768, h16),
+    "Xps": sb(768, bf), "Xpl": sb(768, bf), "JOs": sb(768, h16), "JOl": sb(768, h16), "SEs": sb(768, bf), "SEl": sb(768, bf),
+    "PKs": sb(1536, h16), "PKl": sb(1536, h16),
+    "Nv": sb(256, f32), "NBv": sb(256, bf), "NB": sb(256, bf), "nbi": sb(256, i32),
+    "PTg": sb(256, bf), "CTg": sb(256, bf), "PCT": sb(512, bf), "PTb": sb(256, bf),
+    "gt": sb(256, bf), "okw": sb(256, bf), "ok9": sb(128, bf), "ok16": sb(16, f32),
+    "lt": sb(16, f32), "CW": sb(256, bf), "CW9": sb(128, bf), "TabM": sb(256, bf),
+    "Sc": sb(256, bf), "Ss": sb(256, bf), "ZIs": sb(256, bf), "ZIp": sb(256, bf), "ZIu": sb(256, h16), "EXp": sb(256, bf),
+    "CS": sb(256, bf), "CP": sb(256, bf), "FPm": sb(256, bf), "SM": sb(256, bf), "PH": sb(256, f32), "Q": sb(272, f32),
+    "E": sb(272, f32), "OHh": sb(256, bf), "OHa": sb(256, bf), "RQ": sb(272, bf), "Jenc": sb(256, bf),
+    "NN": sb(256, f32), "Dbuf": sb(272, f32), "OD": sb(256, f32), "foeL": sb(16, u16), "ti": sb(16, i32), "ti2": sb(16, i32),
+    "WS": sb(256, f32),
+    "I8": sb(1024, i32, 8), "I8h": sb(1024, h16, 8), "RB": sb(128, h16, 8),
+    "FI": sb(256, i32), "FL": sb(256, i32), "FH": sb(256, i32), "F7": sb(256, i32), "pi": sb(4, i32), "pf": sb(4, f32),
+    "IDb": sb(128, bf), "IDn": sb(128, bf), "IDh": sb(128, h16), "ID2h": sb(128, h16), "ID8k": sb(128, bf), "C33": sb(128, h16),
+    "BO2": sb(256, bf), "BOh": sb(128, h16), "BO8": sb(8, bf), "Bp": sb(8, bf), "MW": sb(256, bf), "IHI": sb(256, bf),
+    "RST": sb(256, bf), "KB": sb(256, bf), "ONES": sb(128, bf), "wti": sb(1, i32), "wtf": sb(1, f32),
+    "WT": sb(8, bf), "pw": sb(128, f32), "pw2": sb(128, f32), "cr": sb(128, f32), "cz": sb(128, f32),
+    "wc": sb(1, f32), "w2c": sb(1, f32), "b1": sb(2, f32), "OUT": sb(1280, f32), "RX": sb(1472, bf),
+}
+BANKS = ("U2", "K1", "K2", "q0", "q1", "q2", "q3", "q4")
+for _b in BANKS:
+    SCRATCH[_b] = ("psum", [128, 512], f32)
+PACKETS = ("aT", "aE", "aX", "aU", "aJ", "aS", "aP", "aR")
+SEMAPHORES = (["sV", "sS", "sP", "sG", "loc"] + ["d%d" % k for k in range(20)]
+              + [p + str(t) for p in PACKETS for t in range(RO)])
+
+
+def rank_program(g, core, T, topo):
+    rank = T.rank_of(core)
+    if rank is None:
+        return
+    tauW, prevW, foeW, nst, a1, w6, w7, base, mth, base2, nbm, wm = [T.WS[:, 16 * i:16 * i + 16] for i in range(12)]
+    q_of = {"V": g.vector, "S": g.scalar, "P": g.tensor, "G": g, "Y": g.sync}
+    cnt = {"sV": 0, "sS": 0, "sP": 0, "sG": 0, "loc": 0}
+    known = {k: {} for k in q_of}
+    snap = {}
+    wr, rd, bank, ndma = {}, {}, {}, [0]
+
+    def need(q, sem, val):
+        k = known[q]
+        if k.get(sem, 0) >= val:
+            return
+        q_of[q].wait_ge(T.sem[sem], val)
+        k[sem] = val
+        for s, v in snap.get((sem, val), {}).items():
+            k[s] = max(k.get(s, 0), v)
+
+    def deps(q, r, w, me):
+        todo = {}
+
+        def add(s, v):
+            todo[s] = max(todo.get(s, 0), v)
+        for x in r:
+            if x in wr:
+                add(*wr[x])
+        for x in w:
+            if x in wr and not (me == "sP" and wr[x][0] == "sP"):
+                add(*wr[x])
+            for s, v in rd.get(x, {}).items():
+                if s != me:
+                    add(s, v)
+        for x in list(r) + list(w):
+            b = x.split(":")[0]
+            if b in BANKS:
+                for s, v in bank.get(b, {}).items():
+                    if s != me:
+                        add(s, v)
+        for s in sorted(todo, key=lambda s: -todo[s]):
+            need(q, s, todo[s])
+
+    def note(r, w, sem, val):
+        for x in w:
+            wr[x] = (sem, val)
+            rd[x] = {}
+        for x in r:
+            rd.setdefault(x, {})[sem] = val
+        for x in list(r) + list(w):
+            b = x.split(":")[0]
+            if b in BANKS:
+                bank.setdefault(b, {})[sem] = val
+
+    def op(q, call, r, w):
+        sem = "s" + q
+        deps(q, r, w, sem)
+        cnt[sem] += 1
+        snap[(sem, cnt[sem])] = dict(known[q])
+        call(q_of[q]).then_inc(T.sem[sem], 1)
+        note(r, w, sem, cnt[sem])
+
+    def dma(q, out, in_, r, w):
+        sem = "d%d" % ndma[0]
+        ndma[0] += 1
+        deps(q, r, w, "")
+        snap[(sem, 16)] = dict(known[q])
+        q_of[q].dma_start(out, in_).then_inc(T.sem[sem], 16)
+        note(r, w, sem, 16)
+
+    def send(dst, arr, out, in_, src, land):
+        deps("G", [src], [], "")
+        rid, pid = topo.addr(dst)[:2]
+        eng = topo.engines(core, dst)[:ENG]
+        g.remote_dma(out, in_, T.sem[arr], T.sem.loc, pid, rid, sum(1 << e for e in eng))
+        cnt["loc"] += len(eng)
+        wr[land] = (arr, len(eng))
+        rd[land] = {}
+
+    def tt(out, a, b, o, r, w):
+        op("V", lambda e: e.tensor_tensor(out=out, in0=a, in1=b, op=o), r, w)
+
+    def ts(out, a, s1, s2, o0, o1, r, w):
+        if o1 is None:
+            op("V", lambda e: e.tensor_scalar(out=out, in0=a, scalar1=s1, scalar2=None, op0=o0), r, w)
+        else:
+            op("V", lambda e: e.tensor_scalar(out=out, in0=a, scalar1=s1, scalar2=s2, op0=o0, op1=o1), r, w)
+
+    def cp(out, a, r, w):
+        op("V", lambda e: e.tensor_copy(out=out, in_=a), r, w)
+
+    def scan(out, d0, d1, o0, o1, r, w, init=0.0):
+        op("V", lambda e: e.tensor_tensor_scan(out=out, data0=d0, data1=d1, initial=init, op0=o0, op1=o1), r, w)
+
+    def act(out, a, r, w, fn=None, **kw):
+        op("S", lambda e: e.activation(out=out, in_=a, func=fn or F.Copy, **kw), r, w)
+
+    def mm(out, l, rh, start, stop, r, w):
+        op("P", lambda e: e.matmul(out=out, lhsT=l, rhs=rh, start=start, stop=stop), r, w)
+
+    def fill(out, c, w):
+        op("V", lambda e: e.memset(out, c), [], w)
+
+    def half(h, at=0):
+        return slice(at + 128 * h, at + 128 * h + 128)
+
+    def to(t):
+        return T.cores[(rank + 1 + t) % N]
+
+    def back(t):
+        return T.cores[(rank - 1 - t) % N]
+
+    dma("Y", T.I8[:, 768:1024], T.tas[:], [], ["I8u"])
+    dma("S", T.I8[:, 0:256], T.tau[:], [], ["I8t"])
+    dma("Y", T.O[:], T.own[:], [], ["O0", "O1"])
+    dma("S", T.I8[:, 256:512], T.prev[:], [], ["I8p"])
+    dma("Y", T.hue0[:], T.hue[:], [], ["hue0"])
+    dma("S", T.I8[:, 512:768], T.foe[:], [], ["I8f"])
+    dma("Y", T.nbi[:], T.nb[:], [], ["nbi"])
+    dma("Y", T.wti[:], T.wt[:], [], ["wti"])
+    for t in (1, 2):
+        hb, s = T["hue%d" % t], 77 * t
+        dma("Y", hb[:, 0:W - s], T.hue[:, s:W], [], ["hue%da" % t])
+        dma("Y", hb[:, W - s:W], T.hue[:, 0:s], [], ["hue%db" % t])
+
+    op("G", lambda e: e.iota(T.pi[:, 0:1], [[0, 1]], 0, 1), [], ["pi0"])
+    op("G", lambda e: e.iota(T.FI[:], [[1, 256]], 0, 0), [], ["FI"])
+    op("G", lambda e: e.iota(T.KB[:], [[0, 16], [-1, 16]], 15, 0, allow_small_or_imprecise_dtypes=True), [], ["KB"])
+    ts(T.pi[:, 1:2], T.pi[:, 0:1], 15, None, A.bitwise_and, None, ["pi0"], ["pi1"])
+    ts(T.pi[:, 2:3], T.pi[:, 0:1], 4, None, A.arith_shift_right, None, ["pi0"], ["pi2"])
+    cp(T.pf[:, 0:3], T.pi[:, 0:3], ["pi0", "pi1", "pi2"], ["pf"])
+    p0, pl, pg = T.pf[:, 0:1], T.pf[:, 1:2], T.pf[:, 2:3]
+    ts(T.FH[:], T.FI[:], 4, None, A.arith_shift_right, None, ["FI"], ["FH"])
+    ts(T.RB[:], T.FH[0:8, 0:128], T.pf[0:8, 0:1], None, A.is_equal, None, ["FH", "pf"], ["RB"])
+    ts(T.FL[:], T.FI[:], 15, None, A.bitwise_and, None, ["FI"], ["FL"])
+    ts(T.IDh[:], T.FI[:, 0:128], p0, None, A.is_equal, None, ["FI", "pf"], ["IDh"])
+    ts(T.ID2h[:], T.IDh[:], 2.0, None, A.mult, None, ["IDh"], ["ID2h"])
+    ts(T.C33[:], T.IDh[:], 0.0, 33.0, A.mult, A.add, ["IDh"], ["C33"])
+    cp(T.I8h[:, 768:1024], T.I8[:, 768:1024], ["I8u"], ["I8hu"])
+    for h in (0, 1):
+        mm(T.q1[:, half(h)], T.I8h[:, half(h, 768)], T.RB[:], True, True, ["I8hu", "RB"], ["q1:u"])
+    ts(T.I8h[:, 0:256], T.I8[:, 0:256], 1.0, None, A.add, None, ["I8t"], ["I8ht"])
+    mm(T.q2[:, 0:256], T.RB[:], T.I8h[:, 0:256], True, True, ["I8ht", "RB"], ["q2:t"])
+    cp(T.uEs[:, 0:256], T.q1[:, 0:256], ["q1:u"], ["uEs0"])
+
+    def v33(reg, key, src, t, ukey):
+        for h in (0, 1):
+            mm(T.q0[:, half(h, reg)], T.IDh[:], T.C33[:], True, False, ["IDh", "C33"], [key])
+            mm(T.q0[:, half(h, reg)], src[:, half(h, 256 * t)], T.ID2h[:], False, True, [ukey, "ID2h"], [key])
+
+    v33(0, "q0:H", T.uEs, 0, "uEs0")
+    send(to(0), "aE0", T.uEl[:, 0:256], T.uEs[:, 0:256], "uEs0", "uEl0")
+    ts(T.MW[:], T.FL[:], pl, None, A.is_equal, None, ["FL", "pf"], ["MW"])
+    ts(T.RST[:], T.FL[:], 0.5, None, A.is_gt, None, ["FL"], ["RST"])
+
+    def to_w(wide, wkey, tile, tkey):
+        tt(tile, wide, T.MW[:], A.mult, [wkey, "MW"], [tkey])
+        scan(T.EXp[:], T.RST[:], tile, A.mult, A.add, ["RST", tkey], ["EXp"])
+
+    def send_targets(t):
+        o = slice(16 * t, 16 * t + 16)
+        ts(T.taus[:, o], tauW, -1.0, None, A.add, None, ["tauW"], ["taus%d" % t])
+        send(to(t), "aT%d" % t, T.taul[:, o], T.taus[:, o], "taus%d" % t, "taul%d" % t)
+
+    to_w(T.q2[:, 0:256], "q2:t", T.SM[:], "SM")
+    cp(tauW, T.EXp[:, 15:256:16], ["EXp"], ["tauW"])
+    send_targets(0)
+
+    def look(h, pr, sh, off, o, okey, vreg, vkey, tag):
+        b = half(h)
+        tt(pr[:, b], o[:, b], T.q0[:, half(h, vreg)], A.mult, [okey, vkey], ["pr" + tag])
+        ts(sh[:, b], pr[:, b], 5, W - 1, A.arith_shift_right, A.bitwise_and, ["pr" + tag], ["sh" + tag])
+        cp(off[:, b], sh[:, b], ["sh" + tag], ["off%s%d" % (tag, h)])
+
+    def gather(e, t, buf, off, tag, i, c0, c1):
+        src = T["hue%d" % t][:, 0:W].indirect(off[:, c0:c1])
+        r = ["off%s%d" % (tag, h) for h in (0, 1) if c0 < 128 * h + 128 and c1 > 128 * h]
+        r += ["hue0"] if t == 0 else ["hue%da" % t, "hue%db" % t]
+        if e == "S":
+            act(buf[:, 16 * c0:16 * c1], src, r, ["x%s%d" % (tag, i)])
+        else:
+            cp(buf[:, 16 * c0:16 * c1], src, r, ["x%s%d" % (tag, i)])
+
+    def home_gathers(t, e):
+        for i, (q, c0, c1) in enumerate(HCH[min(t, 1)]):
+            if q == e:
+                gather(e, t, T.xH, T.offH, "H", i, c0, c1)
+
+    for h in (0, 1):
+        look(h, T.PR, T.SH, T.offH, T.O, "O%d" % h, 0, "q0:H", "H")
+    home_gathers(0, "S")
+
+    ts(T.IHI[:], T.FH[:], pl, None, A.is_equal, None, ["FH", "pf"], ["IHI"])
+    ts(T.I8h[:, 256:768], T.I8[:, 256:768], 1.0, None, A.add, None, ["I8p", "I8f"], ["I8hpf"])
+    mm(T.q3[:], T.RB[:], T.I8h[:, 256:768], True, True, ["I8hpf", "RB"], ["q3:w"])
+    to_w(T.q3[:, 256:512], "q3:w", T.SM[:], "SM")
+    cp(foeW, T.EXp[:, 15:256:16], ["EXp"], ["foeW"])
+    to_w(T.q3[:, 0:256], "q3:w", T.Xps[:, 0:256], "Xps0")
+    cp(prevW, T.EXp[:, 15:256:16], ["EXp"], ["prevW"])
+
+    def send_prevs(t):
+        s = slice(256 * t, 256 * t + 256)
+        send(to(t), "aX%d" % t, T.Xpl[:, s], T.Xps[:, s], "Xps%d" % t, "Xpl%d" % t)
+
+    send_prevs(0)
+    ts(T.IDb[:], T.FI[:, 0:128], p0, None, A.is_equal, None, ["FI", "pf"], ["IDb"])
+    ts(T.Bp[:], T.FI[:, 0:8], pg, 16.0, A.is_equal, A.mult, ["FI", "pf"], ["Bp"])
+    ts(T.F7[:], T.FH[:], 7, None, A.bitwise_and, None, ["FH"], ["F7"])
+    ts(T.BO2[:], T.F7[:], pg, None, A.is_equal, None, ["F7", "pf"], ["BO2"])
+    ts(T.b1[:, 0:1], p0, 1.0, None, A.add, None, ["pf"], ["b10"])
+    ts(T.b1[:, 1:2], p0, 129.0, None, A.add, None, ["pf"], ["b11"])
+    ts(T.NB[:], T.nbi[:], 1.0, None, A.add, None, ["nbi"], ["NB"])
+    ts(T.RQ[:, 0:256], T.FL[:], 14.5, None, A.is_lt, None, ["FL"], ["RQ0"])
+    ts(T.RQ[:, 256:272], T.FL[:, 0:16], 14.5, None, A.is_lt, None, ["FL"], ["RQ1"])
+    fill(T.Q[:], 0.0, ["Q"])
+    fill(T.cr[:], 1.0 / RHO, ["cr"])
+    fill(T.cz[:], 0.0, ["cz"])
+    scan(T.pw[:], T.cr[:], T.cz[:], A.mult, A.add, ["cr", "cz"], ["pw"], init=TOP)
+    tt(T.pw2[:], T.pw[:], T.IDb[:], A.mult, ["pw", "IDb"], ["pw2"])
+    op("V", lambda e: e.tensor_reduce(out=T.wc[:], in_=T.pw2[:], axis=AX.X, op=A.add), ["pw2"], ["wc"])
+    ts(T.w2c[:], T.wc[:], 2.02, None, A.mult, None, ["wc"], ["w2c"])
+    fill(T.ZIs[:], 0.0, ["ZIs"])
+    fill(T.RX[:], 1.0, ["RX"])
+    fill(T.RX[:, 0:1472:16], 0.0, ["RX"])
+
+    def late_constants():
+        ts(T.IDn[:], T.IDb[:], -1.0, None, A.mult, None, ["IDb"], ["IDn"])
+
+    def later_constants():
+        ts(T.BOh[:], T.F7[:, 0:128], pg, None, A.is_equal, None, ["F7", "pf"], ["BOh"])
+        ts(T.BO8[:], T.FI[:, 0:8], pg, None, A.is_equal, None, ["FI", "pf"], ["BO8"])
+        cp(T.wtf[:], T.wti[:], ["wti"], ["wtf"])
+        ts(T.WT[:], T.BO8[:], T.wtf[:, 0:1], None, A.mult, None, ["BO8", "wtf"], ["WT"])
+        fill(T.ONES[:], 1.0, ["ONES"])
+        fill(T.ONE16[:], 1.0 / 16, ["ONE16"])
+        ts(T.ID8k[:], T.IDb[:], 8192.0, None, A.mult, None, ["IDb"], ["ID8k"])
+        fill(T.Dbuf[:], 0.0, ["D", "D0"])
+        fill(T.ZIp[:], 0.0, ["ZIp"])
+        cp(T.ZIu[:], T.ZIp[:], ["ZIp"], ["ZIu"])
+        cp(T.K2[:, 128:384], T.MW[:], ["MW"], ["K2:M"])
+
+    def pick(kap, kkey, c0, c1, oh, okey):
+        scan(T.PH[:, c0:c1], T.RST[:, c0:c1], kap, A.mult, A.max, ["RST", kkey], ["PH"])
+        cp(T.Q[:, c0 + 15:c1:16], T.PH[:, c0 + 15:c1:16], ["PH"], ["Q"])
+        scan(T.E[:, c0:c1 + 15], T.RQ[:, c0:c1 + 15], T.Q[:, c0:c1 + 15], A.mult, A.add, ["RQ0", "RQ1", "Q"], ["E"])
+        tt(oh[:, c0:c1], T.E[:, c0 + 15:c1 + 15], kap, A.is_equal, ["E", kkey], [okey])
+
+    def own_place(x, k, tile, tkey):
+        cp(T.ZIp[:, 0:256:16], x, [k], ["ZIp"])
+        scan(T.EXp[:], T.RST[:], T.ZIp[:], A.mult, A.add, ["RST", "ZIp"], ["EXp"])
+        tt(tile, T.EXp[:], T.K2[:, 128:384], A.mult, ["EXp", "K2:M"], [tkey])
+
+    def output(x, k, i, ps, pk):
+        own_place(x, k, T.SM[:], "SM")
+        mm(ps, T.BO2[:, 0:128], T.SM[:], True, True, ["BO2", "SM"], [pk])
+        act(T.OUT[:, 256 * i:256 * i + 256], ps, [pk], ["out%d" % i], F.Identity, bias=-1.0)
+
+    for t in range(RO):
+        s = slice(256 * t, 256 * t + 256)
+        last = t == RO - 1
+        Us, Ul, SEs, SEl, tau = T.Us[:, s], T.Ul[:, s], T.SEs[:, s], T.SEl[:, s], T.taul[:, 16 * t:16 * t + 16]
+        tl, kU = "taul%d" % t, "Ul%d" % t
+        v33(256, "q0:A", T.uEl, t, "uEl%d" % t)
+        cp(T.Nv[:], T.O[:].indirect(tau), ["O0", "O1", tl], ["Nv"])
+        for h in (0, 1):
+            look(h, T.PA, T.SA, T.offA, T.Nv, "Nv", 256, "q0:A", "A")
+        act(T.PTg[:], T.MW[:].indirect(tau), ["MW", tl], ["PTg"])
+        act(T.CTg[:], T.IHI[:].indirect(tau), ["IHI", tl], ["CTg"])
+        for i in HORD[min(t, 1)]:
+            c0, c1 = HCH[min(t, 1)][i][1:]
+            scan(T.xP[:, 16 * c0:16 * c1], T.RX[:, 0:16 * (c1 - c0)], T.xH[:, 16 * c0:16 * c1], A.mult, A.max, ["RX", "xH%d" % i], ["xP%d" % i])
+        cp(Us, T.xP[:, 15:4096:16], ["xP0", "xP1", "xP2"], ["Us%d" % t])
+        send(to(t), "aU%d" % t, Ul, Us, "Us%d" % t, kU)
+        if t == 0:
+            late_constants()
+        for h in (0, 1):
+            mm(T.q2[:, half(h)], T.PTg[:, half(h)], T.IDb[:], True, True, ["PTg", "IDb"], ["q2:D"])
+            mm(T.q2[:, half(h, 256)], T.CTg[:, half(h)], T.IDb[:], True, True, ["CTg", "IDb"], ["q2:D"])
+        gather("S", t, T.xA, T.offA, "A", 0, 0, 128)
+        act(T.PCT[:], T.q2[:], ["q2:D"], ["PCT"])
+        for h in (0, 1):
+            act(T.PTb[:, half(h)], T.q2[:, half(h)], ["q2:D", "b1%d" % h], ["PTb%d" % h], scale=T.b1[:, h:h + 1])
+        gather("S", t, T.xA, T.offA, "A", 1, 128, 256)
+        mm(T.U2[:, 0:256], T.IDb[:], Us, True, True, ["IDb", "Us%d" % t], ["U2:H"])
+        mm(T.K1[:, 0:256], T.IDb[:], T.KB[:], True, False, ["IDb", "KB"], ["K1:H"])
+        for k in range(16):
+            tt(T.ZH[:, 256 * k:256 * k + 256], T.xH[:, k:4096:16], T.U2[:, 0:256], A.not_equal, ["xH0", "xH1", "xH2", "U2:H"], ["ZH%d" % k])
+            for h in (0, 1):
+                mm(T.K1[:, 128 * h + k:128 * h + 128:16], T.ZH[:, half(h, 256 * k)], T.Bp[:], False, (k, h) == (15, 1), ["ZH%d" % k, "Bp"], ["K1:H"])
+        op("V", lambda e: e.tensor_tensor(out=T.gt[:], in0=Us.indirect(tau), in1=Ul, op=A.is_gt), ["Us%d" % t, tl, kU], ["gt"])
+        for h in (0, 1):
+            mm(T.q3[:, half(h)], T.gt[:, half(h)], T.BO2[:, 0:128], True, True, ["gt", "BO2"], ["q3:c"])
+        for h in (0, 1):
+            mm(T.q3[:, half(h, 256)], T.Xpl[:, half(h, 256 * t)], T.BO2[:, 0:128], True, True, ["Xpl%d" % t, "BO2"], ["q3:p"])
+        mm(T.U2[:, 256:512], T.IDb[:], Ul, True, True, ["IDb", kU], ["U2:A"])
+        pick(T.K1[:, 0:256], "K1:H", 0, 256, T.OHh, "OHh")
+        for h in (0, 1):
+            mm(T.q1[:, half(h)], T.OHh[:, half(h)], T.IDb[:], True, True, ["OHh", "IDb"], ["q1:o"])
+        ts(T.okw[:], T.q3[:, 0:256], 7.5, T.wc[:, 0:1], A.is_lt, A.mult, ["q3:c", "wc"], ["okw"])
+        ts(T.ok9[:], T.q3[:, 0:128], 7.5, BIG, A.is_lt, A.mult, ["q3:c"], ["ok9"])
+        tt(T.CW[:], T.q2[:, 256:512], T.okw[:], A.mult, ["q2:D", "okw"], ["CW"])
+        tt(T.CW9[:], T.q2[:, 256:384], T.ok9[:], A.mult, ["q2:D", "ok9"], ["CW9"])
+        ts(T.ok16[:], T.q3[:, 0:256:16], 7.5, None, A.is_lt, None, ["q3:c"], ["ok16"])
+        tt(T.JOs[:, s], T.q1[:, 0:256], T.O[:], A.mult, ["q1:o", "O0", "O1"], ["JOs%d" % t])
+        send(to(t), "aJ%d" % t, T.JOl[:, s], T.JOs[:, s], "JOs%d" % t, "JOl%d" % t)
+        act(T.Jenc[:], T.q1[:, 0:256], ["q1:o"], ["Jenc"], scale=12288.0, bias=-16384.0)
+        KA = (T.K2, T.K1)
+        kk = ("K2:A", "K1:A")
+        mine = {h: [k for k in range(16) if not any(o == h and f <= k < f + 4 for o, f in OFF)] for h in (0, 1)}
+
+        def by_scalar(i):
+            h, f = OFF[i]
+            for j in range(4):
+                mm(T.q0[:, half(j)], T.IDb[:], T.xA[:, 2048 * h + f + j:2048 * h + 2048:16], True, False, ["IDb", "xA%d" % h], ["q0:d"])
+                mm(T.q0[:, half(j)], T.IDn[:], T.Ul[:, half(h, 256 * t)], False, True, ["IDn", kU], ["q0:d"])
+            act(T.ZB[:, 512 * i:512 * i + 512], T.q0[:], ["q0:d"], ["ZB%d" % i], F.Relu)
+
+        def open_keys(h):
+            mm(KA[h][:, 0:128], T.IDb[:], T.KB[:, 0:128], True, False, ["IDb", "KB"], [kk[h]])
+
+        def add_scalar(i):
+            h, f = OFF[i]
+            for j in range(4):
+                k = f + j
+                mm(KA[h][:, k:128:16], T.Ul[:, half(h, 256 * t)], T.Bp[:], False, False, [kU, "Bp"], [kk[h]])
+                mm(KA[h][:, k:128:16], T.ZB[:, half(j, 512 * i)], T.Bp[:], False, False, ["ZB%d" % i, "Bp"], [kk[h]])
+
+        def score(h, a, b):
+            for k in mine[h][a:b]:
+                z = T.ZA[:, half(h, 256 * k)]
+                tt(z, T.xA[:, 2048 * h + k:2048 * h + 2048:16], T.U2[:, half(h, 256)], A.max, ["xA%d" % h, "U2:A"], ["ZA%d_%d" % (h, k)])
+                mm(KA[h][:, k:128:16], z, T.Bp[:], False, k == mine[h][-1], ["ZA%d_%d" % (h, k), "Bp"], [kk[h]])
+
+        def best(h):
+            pick(KA[h][:, 0:128], kk[h], 128 * h, 128 * h + 128, T.OHa, "OHa%d" % h)
+            mm(T.q1[:, half(h)], T.OHa[:, half(h)], T.IDb[:], True, True, ["OHa%d" % h, "IDb"], ["q1:o"])
+
+        def loot(h):
+            p = 512 * t + 256 * h
+            tt(T.PKs[:, p:p + 128], T.q1[:, half(h)], T.Nv[:, half(h)], A.mult, ["q1:o", "Nv"], ["PKs%d%d" % (t, h)])
+            tt(T.PKs[:, p + 128:p + 256], T.q1[:, half(h)], T.NBv[:, half(h)], A.mult, ["q1:o", "NBv"], ["PKs%d%d" % (t, h)])
+            send(back(t), "aPaR"[2 * h:2 * h + 2] + str(t), T.PKl[:, p:p + 256], T.PKs[:, p:p + 256], "PKs%d%d" % (t, h), "PKl%d%d" % (t, h))
+
+        by_scalar(0)
+        mm(T.q4[:, 0:128], T.PCT[:, 0:128], T.CW[:, 0:128], True, True, ["PCT", "CW"], ["q4:T"])
+        mm(T.q4[:, 128:256], T.PCT[:, 0:128], T.CW9[:], True, False, ["PCT", "CW9"], ["q4:T"])
+        mm(T.q4[:, 128:256], T.PCT[:, 128:256], T.CW[:, 128:256], False, True, ["PCT", "CW"], ["q4:T"])
+        open_keys(0)
+        score(0, 0, 4)
+        tt(T.TabM[:], T.q4[:, 0:256], T.BO2[:], A.mult, ["q4:T", "BO2"], ["TabM"])
+        for h in (0, 1):
+            mm(T.q4[:, half(h, 256)], T.PTg[:, half(h)], T.TabM[:, half(h)], True, True, ["PTg", "TabM"], ["q4:S"])
+        add_scalar(0)
+        score(0, 4, 6)
+        tt(T.Sc[:], T.q4[:, 256:512], T.PCT[:, 256:512], A.mult, ["q4:S", "PCT"], ["Sc"])
+        score(0, 6, 7)
+        scan(T.Ss[:], T.RST[:], T.Sc[:], A.mult, A.add, ["RST", "Sc"], ["Ss"])
+        by_scalar(1)
+        act(T.NBv[:], T.NB[:].indirect(tau), ["NB", tl], ["NBv"])
+        score(0, 7, 8)
+        ts(T.lt[:], T.Ss[:, 15:256:16], T.w2c[:, 0:1], None, A.is_lt, None, ["Ss", "w2c"], ["lt"])
+        score(0, 8, 9)
+        tt(T.ZIs[:, 0:256:16], T.lt[:], T.ok16[:], A.mult, ["lt", "ok16"], ["ZIs"])
+        score(0, 9, 10)
+        scan(SEs, T.RST[:], T.ZIs[:], A.mult, A.add, ["RST", "ZIs"], ["SEs%d" % t])
+        send(back(t), "aS%d" % t, SEl, SEs, "SEs%d" % t, "SEl%d" % t)
+        score(0, 10, 16)
+        tt(T.CS[:], T.q2[:, 256:512], SEs, A.mult, ["q2:D", "SEs%d" % t], ["CS"])
+        open_keys(1)
+        score(1, 0, 2)
+        best(0)
+        tt(T.CP[:], T.q3[:, 256:512], T.CS[:], A.mult, ["q3:p", "CS"], ["CP"])
+        score(1, 2, 4)
+        loot(0)
+        for h in (0, 1):
+            mm(T.q3[:, 0:128], T.PTb[:, half(h)], T.CS[:, half(h)], h == 0, h == 1, ["PTb%d" % h, "CS"], ["q3:F"])
+        for h in (0, 1):
+            mm(T.q3[:, 128:256], T.PCT[:, half(h)], T.CP[:, half(h)], h == 0, h == 1, ["PCT", "CP"], ["q3:F"])
+        if t == 0:
+            later_constants()
+        add_scalar(1)
+        score(1, 4, 8)
+        tt(T.FPm[:], T.q3[:, 0:256], T.BO2[:], A.mult, ["q3:F", "BO2"], ["FPm"])
+        score(1, 8, 16)
+        best(1)
+        for x in (0, 1):
+            for gg in range(8):
+                mm(T.q3[:, 256 + 16 * x:272 + 16 * x], T.IDb[:], T.FPm[:, 128 * x + 16 * gg:128 * x + 16 * gg + 16], gg == 0, gg == 7,
+                   ["IDb", "FPm"], ["q3:W"])
+        loot(1)
+
+        FW, PW, FPW, sw = T.q3[:, 256:272], T.q3[:, 272:288], T.q3[:, 256:288], T.q0[:, 272:288]
+        mm(T.q1[:, 256:512], T.BOh[:], T.JOl[:, s], True, True, ["BOh", "JOl%d" % t], ["q1:n"])
+        act(T.NN[:], T.q1[:, 256:512], ["q1:n"], ["NN"], F.Identity, bias=8192.0)
+        cp(T.foeL[:], FW, ["q3:W"], ["foeL"])
+        tt(T.SM[:], SEl, T.K2[:, 128:384], A.mult, ["SEl%d" % t, "K2:M"], ["SM"])
+        ts(nst, FW, 0.5, None, A.is_lt, None, ["q3:W"], ["nst"])
+        tt(w7, tauW, prevW, A.subtract, ["tauW", "prevW"], ["w7"])
+        XR = (T.q4, T.q2)
+        for h in (0, 1):
+            mm(XR[h][:, 0:128], T.IDb[:], T.Jenc[:, half(h)], True, False, ["IDb", "Jenc"], [("q4:X", "q2:X")[h]])
+            mm(XR[h][:, 0:128], T.SEl[:, half(h, 256 * t)], T.ID8k[:], False, False, ["SEl%d" % t, "ID8k"], [("q4:X", "q2:X")[h]])
+        for h in (0, 1):
+            mm(T.q0[:, 288:304], T.SEs[:, half(h, 256 * t)], T.ONES[:, 0:16], h == 0, h == 1, ["SEs%d" % t, "ONES"], ["q0:g"])
+        for h in (0, 1):
+            mm(T.q0[:, 272 + 8 * h:280 + 8 * h], T.SM[:, half(h)], T.BO8[:], True, True, ["SM", "BO8"], ["q0:s"])
+        act(T.cg[:], T.q0[:, 288:304], ["q0:g"], ["cg"])
+        mm(T.q0[:, 256:272], T.ONE16[:], T.cg[:], True, False, ["ONE16", "cg"], ["q0:t"])
+        for h in (0, 1):
+            mm(T.q0[:, 256 + 8 * h:264 + 8 * h], T.Us[:, half(h, 256 * t)], T.WT[:], False, h == 1, ["Us%d" % t, "WT"], ["q0:t"])
+        tt(T.Dbuf[:, 1:257], T.q1[:, 0:256], T.NN[:], A.mult, ["q1:o", "NN"], ["D"])
+        tt(a1, foeW, nst, A.mult, ["foeW", "nst"], ["a1"])
+        cp(T.ti[:], T.q0[:, 256:272], ["q0:t"], ["ti"])
+        op("V", lambda e: e.tensor_tensor(out=T.OD[:], in0=T.Dbuf[:].indirect(T.foeL[:]), in1=T.O[:], op=A.max), ["D", "D0", "foeL", "O0", "O1"], ["OD"])
+        tt(mth, sw, nst, A.mult, ["q0:s", "nst"], ["mth"])
+        ts(T.ti2[:], T.ti[:], 1023, None, A.bitwise_and, None, ["ti"], ["ti2"])
+        tt(base, PW, a1, A.add, ["q3:W", "a1"], ["base"])
+        tt(w6, sw, w7, A.mult, ["q0:s", "w7"], ["w6"])
+        cp(T.ZIu[:, 0:256:16], T.ti2[:], ["ti2"], ["ZIu"])
+        tt(foeW, FW, a1, A.add, ["q3:W", "a1"], ["foeW"])
+        tt(wm, mth, base, A.mult, ["mth", "base"], ["wm"])
+        scan(T.uEs[:, 256 * t + 256:256 * t + 512], T.RST[:], T.ZIu[:], A.mult, A.add, ["RST", "ZIu"], ["uEs%d" % (t + 1)])
+        tt(prevW, prevW, w6, A.add, ["prevW", "w6"], ["prevW"])
+        tt(base2, base, wm, A.subtract, ["base", "wm"], ["base2"])
+        if not last:
+            v33(0, "q0:H", T.uEs, t + 1, "uEs%d" % (t + 1))
+            s1 = slice(256 * t + 256, 256 * t + 512)
+            send(to(t + 1), "aE%d" % (t + 1), T.uEl[:, s1], T.uEs[:, s1], "uEs%d" % (t + 1), "uEl%d" % (t + 1))
+            own_place(prevW, "prevW", T.Xps[:, s1], "Xps%d" % (t + 1))
+            send_prevs(t + 1)
+        else:
+            for h in (0, 1):
+                mm(T.q0[:, half(h)], T.uEs[:, half(h, 256 * t + 256)], T.IDh[:], True, True, ["uEs%d" % (t + 1), "IDh"], ["q0:H"])
+            act(T.OUT[:, 1024:1280], T.q0[:, 0:256], ["q0:H"], ["out4"])
+            for i, (x, k) in enumerate(((prevW, "prevW"), (foeW, "foeW"))):
+                output(x, k, 2 + i, T.U2[:, 256 * i:256 * i + 256], "U2:%d" % i)
+            for i, y in ((4, T.yu), (2, T.yp), (3, T.yf)):
+                dma("Y", y[:], T.OUT[0:128:16, 256 * i:256 * i + 256], ["out%d" % i], [])
+        for h in (0, 1):
+            p = 512 * t + 256 * h
+            mm(XR[h][:, 0:128], T.BOh[:], T.PKl[:, p:p + 128], False, True, ["BOh", "PKl%d%d" % (t, h)], [("q4:X", "q2:X")[h]])
+        for h in (0, 1):
+            p = 512 * t + 256 * h
+            mm(T.q3[:, half(h, 256)], T.BOh[:], T.PKl[:, p + 128:p + 256], True, True, ["BOh", "PKl%d%d" % (t, h)], ["q3:n"])
+        for h in (0, 1):
+            tt(T.X1[:, half(h)], XR[h][:, 0:128], T.OD[:, half(h)], A.max, [("q4:X", "q2:X")[h], "OD"], ["X1"])
+            ts(T.O[:, half(h)], T.X1[:, half(h)], W - 1, None, A.bitwise_and, None, ["X1"], ["O%d" % h])
+            if not last:
+                look(h, T.PR, T.SH, T.offH, T.O, "O%d" % h, 0, "q0:H", "H")
+            else:
+                cp(T.OUT[:, half(h)], T.O[:, half(h)], ["O%d" % h], ["out0"])
+        if last:
+            dma("Y", T.yo[:], T.OUT[:, 0:256], ["out0"], [])
+        else:
+            home_gathers(t + 1, "S")
+        to_w(T.q3[:, 256:512], "q3:n", T.SM[:], "SM")
+        tt(nbm, T.EXp[:, 15:256:16], mth, A.mult, ["EXp", "mth"], ["nbm"])
+        tt(tauW, nbm, base2, A.add, ["nbm", "base2"], ["tauW"])
+        if last:
+            output(tauW, "tauW", 1, T.U2[:, 0:256], "U2:0")
+            dma("S", T.yt[:], T.OUT[0:128:16, 256:512], ["out1"], [])
+        else:
+            send_targets(t + 1)
+            home_gathers(t + 1, "V")
+
+    for k in sorted(cnt):
+        if cnt[k]:
+            need("G", k, cnt[k])
+    for k in range(ndma[0]):
+        need("G", "d%d" % k, 16)
+    for x in sorted(wr):
+        if wr[x][0][0] == "a":
+            need("G", *wr[x])

@@ -1,11 +1,10 @@
 from concourse.mybir import AluOpType as A, ActivationFunctionType as F, AxisListType as AX
 
 N, RO, W = 8, 3, 2048
-BIG, TOP, RHO = float(2 ** 90), float(2 ** 74), 2.25
-HCH = [[("S", 0, 88), ("S", 88, 176), ("S", 176, 256)],
-       [("S", 0, 92), ("S", 92, 184), ("V", 184, 256)]]
-HORD = [(0, 1, 2), (2, 0, 1)]
-OFF = [(0, 12), (1, 12)]
+LIFT, TOP, RHO = float(2 ** 48), float(2 ** 74), 2.25
+HCH = [[("S", 0, 64), ("S", 64, 128), ("S", 128, 208), ("V", 208, 256)],
+       [("S", 0, 88), ("V", 88, 128), ("S", 128, 216), ("V", 216, 256)]]
+OFF = [(1, 12)]
 ENG = 16
 
 f32, bf, h16, i32, u16 = "float32", "bfloat16", "float16", "int32", "uint16"
@@ -25,8 +24,7 @@ SCRATCH = {
     "PKs": sb(1536, h16), "PKl": sb(1536, h16),
     "Nv": sb(256, f32), "NBv": sb(256, bf), "NB": sb(256, bf), "nbi": sb(256, i32),
     "PTg": sb(256, bf), "CTg": sb(256, bf), "PCT": sb(512, bf), "PTb": sb(256, bf),
-    "gt": sb(256, bf), "okw": sb(256, bf), "ok9": sb(128, bf), "ok16": sb(16, f32),
-    "lt": sb(16, f32), "CW": sb(256, bf), "CW9": sb(128, bf), "TabM": sb(256, bf),
+    "gt": sb(256, bf), "okw": sb(256, bf), "CW": sb(256, bf), "PTx": sb(128, bf), "TabM": sb(256, bf),
     "Sc": sb(256, bf), "Ss": sb(256, bf), "ZIs": sb(256, bf), "ZIp": sb(256, bf), "ZIu": sb(256, h16), "EXp": sb(256, bf),
     "CS": sb(256, bf), "CP": sb(256, bf), "FPm": sb(256, bf), "SM": sb(256, bf), "PH": sb(256, f32), "Q": sb(272, f32),
     "E": sb(272, f32), "OHh": sb(256, bf), "OHa": sb(256, bf), "RQ": sb(272, bf), "Jenc": sb(256, bf),
@@ -38,14 +36,98 @@ SCRATCH = {
     "BO2": sb(256, bf), "BOh": sb(128, h16), "BO8": sb(8, bf), "Bp": sb(8, bf), "MW": sb(256, bf), "IHI": sb(256, bf),
     "RST": sb(256, bf), "KB": sb(256, bf), "ONES": sb(128, bf), "wti": sb(1, i32), "wtf": sb(1, f32),
     "WT": sb(8, bf), "pw": sb(128, f32), "pw2": sb(128, f32), "cr": sb(128, f32), "cz": sb(128, f32),
-    "wc": sb(1, f32), "w2c": sb(1, f32), "b1": sb(2, f32), "OUT": sb(1280, f32), "RX": sb(1472, bf),
+    "wc": sb(2, f32), "w2c": sb(1, f32), "b1": sb(2, f32), "OUT": sb(1280, f32), "RX": sb(1408, bf),
 }
 BANKS = ("U2", "K1", "K2", "q0", "q1", "q2", "q3", "q4")
 for _b in BANKS:
     SCRATCH[_b] = ("psum", [128, 512], f32)
-PACKETS = ("aT", "aE", "aX", "aU", "aJ", "aS", "aP", "aR")
+PACKETS = ("aT", "aE", "aX", "aU", "aV", "aJ", "aS", "aP", "aR")
 SEMAPHORES = (["sV", "sS", "sP", "sG", "loc"] + ["d%d" % k for k in range(20)]
               + [p + str(t) for p in PACKETS for t in range(RO)])
+
+
+TIME = {
+    "V": {"": .21, "pi": .05, "pf": .05, "RB": .11, "ID": .11, "C33": .05, "I8hpf": .42, "EXp": .08, "tauW": .05, "prevW": .05, "foeW": .05,
+          "nst": .05, "a1": .05, "w": .05, "base": .05, "mth": .05, "nbm": .05, "taus": .05, "pr": .11, "sh": .11, "off": .11, "Bp": .05,
+          "b1": .05, "wc0": .11, "w2c": .2, "ZIs": .05, "RX": .05, "xP": .45, "Us": .05, "xH": 1., "Nv": .37, "gt": .37, "ZA": .11,
+          "okw": .11, "Ss": .11, "SEs": .11, "OHa": .11, "PKs": .11, "BO8": .05, "WT": .05, "ZI": .06, "ti": .05, "foeL": .05, "OD": .37,
+          "X1": .11, "O": .11, "OHh": .21, "uEs1": .11, "uEs2": .11, "uEs3": .11, "PH": .14, "Q": .05, "E": .15, "out": .11},
+    "S": {"": .2, "xH": 1.5, "xA": 2.6, "PTg": .38, "CTg": .38, "NBv": .38, "ZB": .42},
+    "P": {"": .11, "K": .053, "q3:W": .053, "q0:t": .053, "q0:s": .053, "q0:g": .053, "U2": .11}, "G": {"": .5}}
+SELF, WAKE, HOP, LOAD = .2, .25, 3.0, 2.2
+
+
+def cost(q, key):
+    return TIME[q][max((k for k in TIME[q] if key.startswith(k)), key=len)] * 1.1
+
+
+def plan(prog):
+    n = len(prog)
+    succ, npred = [[] for _ in range(n)], [0] * n
+    wr, rd, bank = {}, {}, {}
+    for j, (kind, q, _, r, w, _c) in enumerate(prog):
+        edge = {}
+
+        def after(i, wait):
+            edge[i] = max(edge.get(i, 0.), wait)
+
+        def result(i):
+            ki, qi = prog[i][0], prog[i][1]
+            return HOP if ki == "send" else LOAD if ki == "dma" else (0. if q == "P" else SELF) if qi == q else WAKE
+        for x in r:
+            if x in wr:
+                after(wr[x], result(wr[x]))
+        for x in w:
+            if x in wr:
+                after(wr[x], result(wr[x]))
+            for i in rd.get(x, ()):
+                after(i, SELF if prog[i][1] == q else WAKE)
+        for b in {x.split(":")[0] for x in list(r) + list(w)}:
+            if b in BANKS:
+                runs = bank.setdefault(b, [])
+                if not runs or runs[-1][0] != q:
+                    runs.append((q, []))
+                for i in (runs[-2][1] if len(runs) > 1 else []):
+                    after(i, WAKE)
+                if q == "P" and runs[-1][1]:
+                    after(runs[-1][1][-1], 0.)
+                runs[-1][1].append(j)
+        for x in w:
+            wr[x], rd[x] = j, []
+        for x in r:
+            rd.setdefault(x, []).append(j)
+        edge.pop(j, None)
+        for i, wait in edge.items():
+            succ[i].append((j, wait))
+            npred[j] += 1
+    prio = [0.] * n
+    for i in range(n - 1, -1, -1):
+        prio[i] = prog[i][5] + max([0.] + [wait + prio[j] for j, wait in succ[i]])
+    free = {q: 0. for q in "VSPGY"}
+    ready = {q: [] for q in free}
+    at, order = [0.] * n, []
+    for i in range(n):
+        if npred[i] == 0:
+            ready[prog[i][1]].append(i)
+    while len(order) < n:
+        best = None
+        for q, l in ready.items():
+            if l:
+                start = max(free[q], min(at[i] for i in l))
+                i = max((i for i in l if at[i] <= start + .01), key=lambda i: (prio[i], -i))
+                start = max(start, at[i])
+                if best is None or start < best[0]:
+                    best = (start, q, i)
+        start, q, i = best
+        ready[q].remove(i)
+        order.append(i)
+        free[q] = start + prog[i][5]
+        for j, wait in succ[i]:
+            at[j] = max(at[j], free[q] + wait)
+            npred[j] -= 1
+            if npred[j] == 0:
+                ready[prog[j][1]].append(j)
+    return order
 
 
 def rank_program(g, core, T, topo):
@@ -80,8 +162,7 @@ def rank_program(g, core, T, topo):
             if x in wr and not (me == "sP" and wr[x][0] == "sP"):
                 add(*wr[x])
             for s, v in rd.get(x, {}).items():
-                if s != me:
-                    add(s, v)
+                add(s, v)
         for x in list(r) + list(w):
             b = x.split(":")[0]
             if b in BANKS:
@@ -102,30 +183,41 @@ def rank_program(g, core, T, topo):
             if b in BANKS:
                 bank.setdefault(b, {})[sem] = val
 
+    prog = []
+
     def op(q, call, r, w):
-        sem = "s" + q
-        deps(q, r, w, sem)
-        cnt[sem] += 1
-        snap[(sem, cnt[sem])] = dict(known[q])
-        call(q_of[q]).then_inc(T.sem[sem], 1)
-        note(r, w, sem, cnt[sem])
+        prog.append(("op", q, call, r, w, cost(q, w[0])))
 
     def dma(q, out, in_, r, w):
-        sem = "d%d" % ndma[0]
-        ndma[0] += 1
-        deps(q, r, w, "")
-        snap[(sem, 16)] = dict(known[q])
-        q_of[q].dma_start(out, in_).then_inc(T.sem[sem], 16)
-        note(r, w, sem, 16)
+        prog.append(("dma", q, (out, in_), r, w, 0.1))
 
     def send(dst, arr, out, in_, src, land):
-        deps("G", [src], [], "")
-        rid, pid = topo.addr(dst)[:2]
-        eng = topo.engines(core, dst)[:ENG]
-        g.remote_dma(out, in_, T.sem[arr], T.sem.loc, pid, rid, sum(1 << e for e in eng))
-        cnt["loc"] += len(eng)
-        wr[land] = (arr, len(eng))
-        rd[land] = {}
+        prog.append(("send", "G", (dst, arr, out, in_), [src], [land], 1.0))
+
+    def issue(kind, q, what, r, w):
+        if kind == "op":
+            sem = "s" + q
+            deps(q, r, w, sem)
+            cnt[sem] += 1
+            snap[(sem, cnt[sem])] = dict(known[q])
+            what(q_of[q]).then_inc(T.sem[sem], 1)
+            note(r, w, sem, cnt[sem])
+        elif kind == "dma":
+            sem = "d%d" % ndma[0]
+            ndma[0] += 1
+            deps(q, r, w, "")
+            snap[(sem, 16)] = dict(known[q])
+            q_of[q].dma_start(*what).then_inc(T.sem[sem], 16)
+            note(r, w, sem, 16)
+        else:
+            dst, arr, out, in_ = what
+            deps("G", r, [], "")
+            rid, pid = topo.addr(dst)[:2]
+            eng = topo.engines(core, dst)[:ENG]
+            g.remote_dma(out, in_, T.sem[arr], T.sem.loc, pid, rid, sum(1 << e for e in eng))
+            cnt["loc"] += len(eng)
+            wr[w[0]] = (arr, len(eng))
+            rd[w[0]] = {}
 
     def tt(out, a, b, o, r, w):
         op("V", lambda e: e.tensor_tensor(out=out, in0=a, in1=b, op=o), r, w)
@@ -218,9 +310,9 @@ def rank_program(g, core, T, topo):
 
     def look(h, pr, sh, off, o, okey, vreg, vkey, tag):
         b = half(h)
-        tt(pr[:, b], o[:, b], T.q0[:, half(h, vreg)], A.mult, [okey, vkey], ["pr" + tag])
-        ts(sh[:, b], pr[:, b], 5, W - 1, A.arith_shift_right, A.bitwise_and, ["pr" + tag], ["sh" + tag])
-        cp(off[:, b], sh[:, b], ["sh" + tag], ["off%s%d" % (tag, h)])
+        tt(pr[:, b], o[:, b], T.q0[:, half(h, vreg)], A.mult, [okey, vkey], ["pr%s%d" % (tag, h)])
+        ts(sh[:, b], pr[:, b], 5, W - 1, A.arith_shift_right, A.bitwise_and, ["pr%s%d" % (tag, h)], ["sh%s%d" % (tag, h)])
+        cp(off[:, b], sh[:, b], ["sh%s%d" % (tag, h)], ["off%s%d" % (tag, h)])
 
     def gather(e, t, buf, off, tag, i, c0, c1):
         src = T["hue%d" % t][:, 0:W].indirect(off[:, c0:c1])
@@ -231,14 +323,32 @@ def rank_program(g, core, T, topo):
         else:
             cp(buf[:, 16 * c0:16 * c1], src, r, ["x%s%d" % (tag, i)])
 
-    def home_gathers(t, e):
-        for i, (q, c0, c1) in enumerate(HCH[min(t, 1)]):
-            if q == e:
-                gather(e, t, T.xH, T.offH, "H", i, c0, c1)
+    def home_gather(t, i):
+        gather(HCH[min(t, 1)][i][0], t, T.xH, T.offH, "H", i, *HCH[min(t, 1)][i][1:])
 
-    for h in (0, 1):
+    def home_look(h):
         look(h, T.PR, T.SH, T.offH, T.O, "O%d" % h, 0, "q0:H", "H")
-    home_gathers(0, "S")
+
+    def home_best(t, h):
+        for i in (2 * h, 2 * h + 1):
+            c0, c1 = HCH[min(t, 1)][i][1:]
+            scan(T.xP[:, 16 * c0:16 * c1], T.RX[:, 0:16 * (c1 - c0)], T.xH[:, 16 * c0:16 * c1], A.mult, A.max, ["RX", "xH%d" % i], ["xP%d" % i])
+        b = half(h, 256 * t)
+        cp(T.Us[:, b], T.xP[:, 2048 * h + 15:2048 * h + 2048:16], ["xP%d" % (2 * h), "xP%d" % (2 * h + 1)], ["Us%d%d" % (t, h)])
+        send(to(t), "aUaV"[2 * h:2 * h + 2] + str(t), T.Ul[:, b], T.Us[:, b], "Us%d%d" % (t, h), "Ul%d%d" % (t, h))
+
+    def const(out, shape, key, c):
+        act(out, shape, ["KB"], [key], scale=0.0, bias=c)
+
+    for i in range(0, 1408, 256):
+        j = min(i + 256, 1408)
+        const(T.RX[:, i:j], T.KB[:, 0:j - i], "RX", 1.0)
+    const(T.cr[:], T.KB[:, 0:128], "cr", 1.0 / RHO)
+    const(T.cz[:], T.KB[:, 0:128], "cz", 0.0)
+    for h in (0, 1):
+        home_look(h)
+    for i in (0, 1, 2):
+        home_gather(0, i)
 
     ts(T.IHI[:], T.FH[:], pl, None, A.is_equal, None, ["FH", "pf"], ["IHI"])
     ts(T.I8h[:, 256:768], T.I8[:, 256:768], 1.0, None, A.add, None, ["I8p", "I8f"], ["I8hpf"])
@@ -262,38 +372,37 @@ def rank_program(g, core, T, topo):
     ts(T.NB[:], T.nbi[:], 1.0, None, A.add, None, ["nbi"], ["NB"])
     ts(T.RQ[:, 0:256], T.FL[:], 14.5, None, A.is_lt, None, ["FL"], ["RQ0"])
     ts(T.RQ[:, 256:272], T.FL[:, 0:16], 14.5, None, A.is_lt, None, ["FL"], ["RQ1"])
-    fill(T.Q[:], 0.0, ["Q"])
-    fill(T.cr[:], 1.0 / RHO, ["cr"])
-    fill(T.cz[:], 0.0, ["cz"])
+    fill(T.Q[:], 0.0, ["Q0", "Q1"])
     scan(T.pw[:], T.cr[:], T.cz[:], A.mult, A.add, ["cr", "cz"], ["pw"], init=TOP)
     tt(T.pw2[:], T.pw[:], T.IDb[:], A.mult, ["pw", "IDb"], ["pw2"])
-    op("V", lambda e: e.tensor_reduce(out=T.wc[:], in_=T.pw2[:], axis=AX.X, op=A.add), ["pw2"], ["wc"])
-    ts(T.w2c[:], T.wc[:], 2.02, None, A.mult, None, ["wc"], ["w2c"])
+    op("V", lambda e: e.tensor_reduce(out=T.wc[:, 0:1], in_=T.pw2[:], axis=AX.X, op=A.add), ["pw2"], ["wc0"])
+    ts(T.wc[:, 1:2], T.wc[:, 0:1], 1 / LIFT, None, A.mult, None, ["wc0"], ["wc1"])
+    op("V", lambda e: e.reciprocal(out=T.w2c[:, 0:1], in_=T.wc[:, 0:1]), ["wc0"], ["w2c"])
+    ts(T.w2c[:, 0:1], T.w2c[:, 0:1], LIFT, None, A.mult, None, ["w2c"], ["wx"])
     fill(T.ZIs[:], 0.0, ["ZIs"])
-    fill(T.RX[:], 1.0, ["RX"])
-    fill(T.RX[:, 0:1472:16], 0.0, ["RX"])
-
-    def late_constants():
-        ts(T.IDn[:], T.IDb[:], -1.0, None, A.mult, None, ["IDb"], ["IDn"])
+    fill(T.RX[:, 0:1408:16], 0.0, ["RX"])
+    const(T.ONES[:], T.KB[:, 0:128], "ONES", 1.0)
+    const(T.ONE16[:], T.KB[:, 0:128], "ONE16", 1.0 / 16)
+    act(T.IDn[:], T.IDb[:], ["IDb"], ["IDn"], scale=-1.0)
+    act(T.ID8k[:], T.IDb[:], ["IDb"], ["ID8k"], scale=8192.0)
 
     def later_constants():
         ts(T.BOh[:], T.F7[:, 0:128], pg, None, A.is_equal, None, ["F7", "pf"], ["BOh"])
         ts(T.BO8[:], T.FI[:, 0:8], pg, None, A.is_equal, None, ["FI", "pf"], ["BO8"])
         cp(T.wtf[:], T.wti[:], ["wti"], ["wtf"])
         ts(T.WT[:], T.BO8[:], T.wtf[:, 0:1], None, A.mult, None, ["BO8", "wtf"], ["WT"])
-        fill(T.ONES[:], 1.0, ["ONES"])
-        fill(T.ONE16[:], 1.0 / 16, ["ONE16"])
-        ts(T.ID8k[:], T.IDb[:], 8192.0, None, A.mult, None, ["IDb"], ["ID8k"])
         fill(T.Dbuf[:], 0.0, ["D", "D0"])
         fill(T.ZIp[:], 0.0, ["ZIp"])
         cp(T.ZIu[:], T.ZIp[:], ["ZIp"], ["ZIu"])
         cp(T.K2[:, 128:384], T.MW[:], ["MW"], ["K2:M"])
 
     def pick(kap, kkey, c0, c1, oh, okey):
-        scan(T.PH[:, c0:c1], T.RST[:, c0:c1], kap, A.mult, A.max, ["RST", kkey], ["PH"])
-        cp(T.Q[:, c0 + 15:c1:16], T.PH[:, c0 + 15:c1:16], ["PH"], ["Q"])
-        scan(T.E[:, c0:c1 + 15], T.RQ[:, c0:c1 + 15], T.Q[:, c0:c1 + 15], A.mult, A.add, ["RQ0", "RQ1", "Q"], ["E"])
-        tt(oh[:, c0:c1], T.E[:, c0 + 15:c1 + 15], kap, A.is_equal, ["E", kkey], [okey])
+        hs = range(c0 // 128, c1 // 128)
+        kp, kq = ["PH%d" % h for h in hs], ["Q%d" % h for h in hs]
+        scan(T.PH[:, c0:c1], T.RST[:, c0:c1], kap, A.mult, A.max, ["RST", kkey], kp)
+        cp(T.Q[:, c0 + 15:c1:16], T.PH[:, c0 + 15:c1:16], kp, kq)
+        scan(T.E[:, c0:c1 + 15], T.RQ[:, c0:c1 + 15], T.Q[:, c0:c1 + 15], A.mult, A.add, ["RQ0", "RQ1"] + kq, ["E0", "E1"])
+        tt(oh[:, c0:c1], T.E[:, c0 + 15:c1 + 15], kap, A.is_equal, ["E0", "E1", kkey], [okey])
 
     def own_place(x, k, tile, tkey):
         cp(T.ZIp[:, 0:256:16], x, [k], ["ZIp"])
@@ -309,60 +418,43 @@ def rank_program(g, core, T, topo):
         s = slice(256 * t, 256 * t + 256)
         last = t == RO - 1
         Us, Ul, SEs, SEl, tau = T.Us[:, s], T.Ul[:, s], T.SEs[:, s], T.SEl[:, s], T.taul[:, 16 * t:16 * t + 16]
-        tl, kU = "taul%d" % t, "Ul%d" % t
+        tl = "taul%d" % t
+        kUs, kUl = ["Us%d0" % t, "Us%d1" % t], ["Ul%d0" % t, "Ul%d1" % t]
+        home_best(t, 0)
+        home_gather(t, 3)
+        home_best(t, 1)
         v33(256, "q0:A", T.uEl, t, "uEl%d" % t)
         cp(T.Nv[:], T.O[:].indirect(tau), ["O0", "O1", tl], ["Nv"])
         for h in (0, 1):
             look(h, T.PA, T.SA, T.offA, T.Nv, "Nv", 256, "q0:A", "A")
         act(T.PTg[:], T.MW[:].indirect(tau), ["MW", tl], ["PTg"])
         act(T.CTg[:], T.IHI[:].indirect(tau), ["IHI", tl], ["CTg"])
-        for i in HORD[min(t, 1)]:
-            c0, c1 = HCH[min(t, 1)][i][1:]
-            scan(T.xP[:, 16 * c0:16 * c1], T.RX[:, 0:16 * (c1 - c0)], T.xH[:, 16 * c0:16 * c1], A.mult, A.max, ["RX", "xH%d" % i], ["xP%d" % i])
-        cp(Us, T.xP[:, 15:4096:16], ["xP0", "xP1", "xP2"], ["Us%d" % t])
-        send(to(t), "aU%d" % t, Ul, Us, "Us%d" % t, kU)
-        if t == 0:
-            late_constants()
+        gather("S", t, T.xA, T.offA, "A", 0, 0, 128)
         for h in (0, 1):
             mm(T.q2[:, half(h)], T.PTg[:, half(h)], T.IDb[:], True, True, ["PTg", "IDb"], ["q2:D"])
             mm(T.q2[:, half(h, 256)], T.CTg[:, half(h)], T.IDb[:], True, True, ["CTg", "IDb"], ["q2:D"])
-        gather("S", t, T.xA, T.offA, "A", 0, 0, 128)
-        act(T.PCT[:], T.q2[:], ["q2:D"], ["PCT"])
+        act(T.PCT[:, 0:256], T.q2[:, 0:256], ["q2:D"], ["PT"])
+        act(T.PCT[:, 256:512], T.q2[:, 256:512], ["q2:D"], ["CT"], scale=1 / 2.02)
+        act(T.PTx[:], T.q2[:, 0:128], ["q2:D", "wx"], ["PTx"], scale=T.w2c[:, 0:1])
         for h in (0, 1):
             act(T.PTb[:, half(h)], T.q2[:, half(h)], ["q2:D", "b1%d" % h], ["PTb%d" % h], scale=T.b1[:, h:h + 1])
         gather("S", t, T.xA, T.offA, "A", 1, 128, 256)
-        mm(T.U2[:, 0:256], T.IDb[:], Us, True, True, ["IDb", "Us%d" % t], ["U2:H"])
+        mm(T.U2[:, 0:256], T.IDb[:], Us, True, True, ["IDb"] + kUs, ["U2:H"])
         mm(T.K1[:, 0:256], T.IDb[:], T.KB[:], True, False, ["IDb", "KB"], ["K1:H"])
         for k in range(16):
-            tt(T.ZH[:, 256 * k:256 * k + 256], T.xH[:, k:4096:16], T.U2[:, 0:256], A.not_equal, ["xH0", "xH1", "xH2", "U2:H"], ["ZH%d" % k])
+            tt(T.ZH[:, 256 * k:256 * k + 256], T.xH[:, k:4096:16], T.U2[:, 0:256], A.not_equal, ["xH0", "xH1", "xH2", "xH3", "U2:H"], ["ZH%d" % k])
             for h in (0, 1):
                 mm(T.K1[:, 128 * h + k:128 * h + 128:16], T.ZH[:, half(h, 256 * k)], T.Bp[:], False, (k, h) == (15, 1), ["ZH%d" % k, "Bp"], ["K1:H"])
-        op("V", lambda e: e.tensor_tensor(out=T.gt[:], in0=Us.indirect(tau), in1=Ul, op=A.is_gt), ["Us%d" % t, tl, kU], ["gt"])
-        for h in (0, 1):
-            mm(T.q3[:, half(h)], T.gt[:, half(h)], T.BO2[:, 0:128], True, True, ["gt", "BO2"], ["q3:c"])
-        for h in (0, 1):
-            mm(T.q3[:, half(h, 256)], T.Xpl[:, half(h, 256 * t)], T.BO2[:, 0:128], True, True, ["Xpl%d" % t, "BO2"], ["q3:p"])
-        mm(T.U2[:, 256:512], T.IDb[:], Ul, True, True, ["IDb", kU], ["U2:A"])
-        pick(T.K1[:, 0:256], "K1:H", 0, 256, T.OHh, "OHh")
-        for h in (0, 1):
-            mm(T.q1[:, half(h)], T.OHh[:, half(h)], T.IDb[:], True, True, ["OHh", "IDb"], ["q1:o"])
-        ts(T.okw[:], T.q3[:, 0:256], 7.5, T.wc[:, 0:1], A.is_lt, A.mult, ["q3:c", "wc"], ["okw"])
-        ts(T.ok9[:], T.q3[:, 0:128], 7.5, BIG, A.is_lt, A.mult, ["q3:c"], ["ok9"])
-        tt(T.CW[:], T.q2[:, 256:512], T.okw[:], A.mult, ["q2:D", "okw"], ["CW"])
-        tt(T.CW9[:], T.q2[:, 256:384], T.ok9[:], A.mult, ["q2:D", "ok9"], ["CW9"])
-        ts(T.ok16[:], T.q3[:, 0:256:16], 7.5, None, A.is_lt, None, ["q3:c"], ["ok16"])
-        tt(T.JOs[:, s], T.q1[:, 0:256], T.O[:], A.mult, ["q1:o", "O0", "O1"], ["JOs%d" % t])
-        send(to(t), "aJ%d" % t, T.JOl[:, s], T.JOs[:, s], "JOs%d" % t, "JOl%d" % t)
-        act(T.Jenc[:], T.q1[:, 0:256], ["q1:o"], ["Jenc"], scale=12288.0, bias=-16384.0)
         KA = (T.K2, T.K1)
         kk = ("K2:A", "K1:A")
+        kA = (["xA0"], ["xA1"])
         mine = {h: [k for k in range(16) if not any(o == h and f <= k < f + 4 for o, f in OFF)] for h in (0, 1)}
 
         def by_scalar(i):
             h, f = OFF[i]
             for j in range(4):
-                mm(T.q0[:, half(j)], T.IDb[:], T.xA[:, 2048 * h + f + j:2048 * h + 2048:16], True, False, ["IDb", "xA%d" % h], ["q0:d"])
-                mm(T.q0[:, half(j)], T.IDn[:], T.Ul[:, half(h, 256 * t)], False, True, ["IDn", kU], ["q0:d"])
+                mm(T.q0[:, half(j)], T.IDb[:], T.xA[:, 2048 * h + f + j:2048 * h + 2048:16], True, False, ["IDb"] + kA[h], ["q0:d"])
+                mm(T.q0[:, half(j)], T.IDn[:], T.Ul[:, half(h, 256 * t)], False, True, ["IDn", kUl[h]], ["q0:d"])
             act(T.ZB[:, 512 * i:512 * i + 512], T.q0[:], ["q0:d"], ["ZB%d" % i], F.Relu)
 
         def open_keys(h):
@@ -372,13 +464,13 @@ def rank_program(g, core, T, topo):
             h, f = OFF[i]
             for j in range(4):
                 k = f + j
-                mm(KA[h][:, k:128:16], T.Ul[:, half(h, 256 * t)], T.Bp[:], False, False, [kU, "Bp"], [kk[h]])
+                mm(KA[h][:, k:128:16], T.Ul[:, half(h, 256 * t)], T.Bp[:], False, False, [kUl[h], "Bp"], [kk[h]])
                 mm(KA[h][:, k:128:16], T.ZB[:, half(j, 512 * i)], T.Bp[:], False, False, ["ZB%d" % i, "Bp"], [kk[h]])
 
         def score(h, a, b):
             for k in mine[h][a:b]:
                 z = T.ZA[:, half(h, 256 * k)]
-                tt(z, T.xA[:, 2048 * h + k:2048 * h + 2048:16], T.U2[:, half(h, 256)], A.max, ["xA%d" % h, "U2:A"], ["ZA%d_%d" % (h, k)])
+                tt(z, T.xA[:, 2048 * h + k:2048 * h + 2048:16], T.U2[:, half(h, 256)], A.max, kA[h] + ["U2:A%d" % h], ["ZA%d_%d" % (h, k)])
                 mm(KA[h][:, k:128:16], z, T.Bp[:], False, k == mine[h][-1], ["ZA%d_%d" % (h, k), "Bp"], [kk[h]])
 
         def best(h):
@@ -391,94 +483,104 @@ def rank_program(g, core, T, topo):
             tt(T.PKs[:, p + 128:p + 256], T.q1[:, half(h)], T.NBv[:, half(h)], A.mult, ["q1:o", "NBv"], ["PKs%d%d" % (t, h)])
             send(back(t), "aPaR"[2 * h:2 * h + 2] + str(t), T.PKl[:, p:p + 256], T.PKs[:, p:p + 256], "PKs%d%d" % (t, h), "PKl%d%d" % (t, h))
 
-        by_scalar(0)
-        mm(T.q4[:, 0:128], T.PCT[:, 0:128], T.CW[:, 0:128], True, True, ["PCT", "CW"], ["q4:T"])
-        mm(T.q4[:, 128:256], T.PCT[:, 0:128], T.CW9[:], True, False, ["PCT", "CW9"], ["q4:T"])
-        mm(T.q4[:, 128:256], T.PCT[:, 128:256], T.CW[:, 128:256], False, True, ["PCT", "CW"], ["q4:T"])
+        for h in (0, 1):
+            mm(T.U2[:, half(h, 256)], T.IDb[:], T.Ul[:, half(h, 256 * t)], True, True, ["IDb", kUl[h]], ["U2:A%d" % h])
+        tt(T.gt[:], Us.indirect(tau), Ul, A.is_gt, kUs + kUl + [tl], ["gt"])
+        for h in (0, 1):
+            mm(T.q3[:, half(h, 256)], T.Xpl[:, half(h, 256 * t)], T.BO2[:, 0:128], True, True, ["Xpl%d" % t, "BO2"], ["q3:p"])
+        for h in (0, 1):
+            mm(T.q3[:, half(h)], T.gt[:, half(h)], T.BO2[:, 0:128], True, True, ["gt", "BO2"], ["q3:c"])
+        pick(T.K1[:, 0:256], "K1:H", 0, 256, T.OHh, "OHh")
+        for h in (0, 1):
+            mm(T.q1[:, half(h)], T.OHh[:, half(h)], T.IDb[:], True, True, ["OHh", "IDb"], ["q1:o"])
+        for h in (0, 1):
+            ts(T.okw[:, half(h)], T.q3[:, half(h)], 7.5, T.wc[:, h:h + 1], A.is_lt, A.mult, ["q3:c", "wc%d" % h], ["okw"])
+        tt(T.CW[:], T.q2[:, 256:512], T.okw[:], A.mult, ["q2:D", "okw"], ["CW"])
+        mm(T.q4[:, 0:128], T.PCT[:, 0:128], T.CW[:, 0:128], True, True, ["PT", "CW"], ["q4:T"])
+        mm(T.q4[:, 128:256], T.PTx[:], T.CW[:, 0:128], True, False, ["PTx", "CW"], ["q4:T"])
+        mm(T.q4[:, 128:256], T.PCT[:, 128:256], T.CW[:, 128:256], False, True, ["PT", "CW"], ["q4:T"])
+        tt(T.JOs[:, s], T.q1[:, 0:256], T.O[:], A.mult, ["q1:o", "O0", "O1"], ["JOs%d" % t])
+        send(to(t), "aJ%d" % t, T.JOl[:, s], T.JOs[:, s], "JOs%d" % t, "JOl%d" % t)
+        act(T.Jenc[:], T.q1[:, 0:256], ["q1:o"], ["Jenc"], scale=12288.0, bias=-16384.0)
+        act(T.NBv[:], T.NB[:].indirect(tau), ["NB", tl], ["NBv"])
         open_keys(0)
-        score(0, 0, 4)
+        score(0, 0, 3)
         tt(T.TabM[:], T.q4[:, 0:256], T.BO2[:], A.mult, ["q4:T", "BO2"], ["TabM"])
         for h in (0, 1):
             mm(T.q4[:, half(h, 256)], T.PTg[:, half(h)], T.TabM[:, half(h)], True, True, ["PTg", "TabM"], ["q4:S"])
-        add_scalar(0)
-        score(0, 4, 6)
-        tt(T.Sc[:], T.q4[:, 256:512], T.PCT[:, 256:512], A.mult, ["q4:S", "PCT"], ["Sc"])
+        score(0, 3, 6)
+        tt(T.Sc[:], T.q4[:, 256:512], T.PCT[:, 256:512], A.mult, ["q4:S", "CT"], ["Sc"])
         score(0, 6, 7)
+        by_scalar(0)
         scan(T.Ss[:], T.RST[:], T.Sc[:], A.mult, A.add, ["RST", "Sc"], ["Ss"])
-        by_scalar(1)
-        act(T.NBv[:], T.NB[:].indirect(tau), ["NB", tl], ["NBv"])
         score(0, 7, 8)
-        ts(T.lt[:], T.Ss[:, 15:256:16], T.w2c[:, 0:1], None, A.is_lt, None, ["Ss", "w2c"], ["lt"])
+        tt(T.ZIs[:, 0:256:16], T.Ss[:, 15:256:16], T.okw[:, 0:256:16], A.is_lt, ["Ss", "okw"], ["ZIs"])
         score(0, 8, 9)
-        tt(T.ZIs[:, 0:256:16], T.lt[:], T.ok16[:], A.mult, ["lt", "ok16"], ["ZIs"])
-        score(0, 9, 10)
         scan(SEs, T.RST[:], T.ZIs[:], A.mult, A.add, ["RST", "ZIs"], ["SEs%d" % t])
         send(back(t), "aS%d" % t, SEl, SEs, "SEs%d" % t, "SEl%d" % t)
-        score(0, 10, 16)
+        score(0, 9, 11)
         tt(T.CS[:], T.q2[:, 256:512], SEs, A.mult, ["q2:D", "SEs%d" % t], ["CS"])
+        score(0, 11, 16)
         open_keys(1)
-        score(1, 0, 2)
-        best(0)
+        score(1, 0, 1)
         tt(T.CP[:], T.q3[:, 256:512], T.CS[:], A.mult, ["q3:p", "CS"], ["CP"])
-        score(1, 2, 4)
-        loot(0)
+        best(0)
         for h in (0, 1):
             mm(T.q3[:, 0:128], T.PTb[:, half(h)], T.CS[:, half(h)], h == 0, h == 1, ["PTb%d" % h, "CS"], ["q3:F"])
         for h in (0, 1):
-            mm(T.q3[:, 128:256], T.PCT[:, half(h)], T.CP[:, half(h)], h == 0, h == 1, ["PCT", "CP"], ["q3:F"])
+            mm(T.q3[:, 128:256], T.PCT[:, half(h)], T.CP[:, half(h)], h == 0, h == 1, ["PT", "CP"], ["q3:F"])
+        score(1, 1, 3)
+        loot(0)
         if t == 0:
             later_constants()
-        add_scalar(1)
-        score(1, 4, 8)
         tt(T.FPm[:], T.q3[:, 0:256], T.BO2[:], A.mult, ["q3:F", "BO2"], ["FPm"])
-        score(1, 8, 16)
+        add_scalar(0)
+        score(1, 3, 16)
         best(1)
+        for h in (0, 1):
+            mm(T.q0[:, 288:304], T.SEs[:, half(h, 256 * t)], T.ONES[:, 0:16], h == 0, h == 1, ["SEs%d" % t, "ONES"], ["q0:g"])
+        act(T.cg[:], T.q0[:, 288:304], ["q0:g"], ["cg"])
+        mm(T.q0[:, 256:272], T.ONE16[:], T.cg[:], True, False, ["ONE16", "cg"], ["q0:t"])
+        for h in (0, 1):
+            mm(T.q0[:, 256 + 8 * h:264 + 8 * h], T.Us[:, half(h, 256 * t)], T.WT[:], False, h == 1, [kUs[h], "WT"], ["q0:t"])
         for x in (0, 1):
             for gg in range(8):
                 mm(T.q3[:, 256 + 16 * x:272 + 16 * x], T.IDb[:], T.FPm[:, 128 * x + 16 * gg:128 * x + 16 * gg + 16], gg == 0, gg == 7,
                    ["IDb", "FPm"], ["q3:W"])
         loot(1)
-
-        FW, PW, FPW, sw = T.q3[:, 256:272], T.q3[:, 272:288], T.q3[:, 256:288], T.q0[:, 272:288]
         mm(T.q1[:, 256:512], T.BOh[:], T.JOl[:, s], True, True, ["BOh", "JOl%d" % t], ["q1:n"])
         act(T.NN[:], T.q1[:, 256:512], ["q1:n"], ["NN"], F.Identity, bias=8192.0)
+        cp(T.ti[:], T.q0[:, 256:272], ["q0:t"], ["ti"])
+        ts(T.ti2[:], T.ti[:], 1023, None, A.bitwise_and, None, ["ti"], ["ti2"])
+        cp(T.ZIu[:, 0:256:16], T.ti2[:], ["ti2"], ["ZIu"])
+        scan(T.uEs[:, 256 * t + 256:256 * t + 512], T.RST[:], T.ZIu[:], A.mult, A.add, ["RST", "ZIu"], ["uEs%d" % (t + 1)])
+        s1 = slice(256 * t + 256, 256 * t + 512)
+        if not last:
+            v33(0, "q0:H", T.uEs, t + 1, "uEs%d" % (t + 1))
+            send(to(t + 1), "aE%d" % (t + 1), T.uEl[:, s1], T.uEs[:, s1], "uEs%d" % (t + 1), "uEl%d" % (t + 1))
+
+        FW, PW, FPW, sw = T.q3[:, 256:272], T.q3[:, 272:288], T.q3[:, 256:288], T.q0[:, 272:288]
         cp(T.foeL[:], FW, ["q3:W"], ["foeL"])
-        tt(T.SM[:], SEl, T.K2[:, 128:384], A.mult, ["SEl%d" % t, "K2:M"], ["SM"])
         ts(nst, FW, 0.5, None, A.is_lt, None, ["q3:W"], ["nst"])
         tt(w7, tauW, prevW, A.subtract, ["tauW", "prevW"], ["w7"])
+        tt(T.Dbuf[:, 1:257], T.q1[:, 0:256], T.NN[:], A.mult, ["q1:o", "NN"], ["D"])
+        tt(a1, foeW, nst, A.mult, ["foeW", "nst"], ["a1"])
+        op("V", lambda e: e.tensor_tensor(out=T.OD[:], in0=T.Dbuf[:].indirect(T.foeL[:]), in1=T.O[:], op=A.max), ["D", "D0", "foeL", "O0", "O1"], ["OD"])
+        tt(base, PW, a1, A.add, ["q3:W", "a1"], ["base"])
+        tt(foeW, FW, a1, A.add, ["q3:W", "a1"], ["foeW"])
+        tt(T.SM[:], SEl, T.K2[:, 128:384], A.mult, ["SEl%d" % t, "K2:M"], ["SM"])
         XR = (T.q4, T.q2)
         for h in (0, 1):
             mm(XR[h][:, 0:128], T.IDb[:], T.Jenc[:, half(h)], True, False, ["IDb", "Jenc"], [("q4:X", "q2:X")[h]])
             mm(XR[h][:, 0:128], T.SEl[:, half(h, 256 * t)], T.ID8k[:], False, False, ["SEl%d" % t, "ID8k"], [("q4:X", "q2:X")[h]])
         for h in (0, 1):
-            mm(T.q0[:, 288:304], T.SEs[:, half(h, 256 * t)], T.ONES[:, 0:16], h == 0, h == 1, ["SEs%d" % t, "ONES"], ["q0:g"])
-        for h in (0, 1):
             mm(T.q0[:, 272 + 8 * h:280 + 8 * h], T.SM[:, half(h)], T.BO8[:], True, True, ["SM", "BO8"], ["q0:s"])
-        act(T.cg[:], T.q0[:, 288:304], ["q0:g"], ["cg"])
-        mm(T.q0[:, 256:272], T.ONE16[:], T.cg[:], True, False, ["ONE16", "cg"], ["q0:t"])
-        for h in (0, 1):
-            mm(T.q0[:, 256 + 8 * h:264 + 8 * h], T.Us[:, half(h, 256 * t)], T.WT[:], False, h == 1, ["Us%d" % t, "WT"], ["q0:t"])
-        tt(T.Dbuf[:, 1:257], T.q1[:, 0:256], T.NN[:], A.mult, ["q1:o", "NN"], ["D"])
-        tt(a1, foeW, nst, A.mult, ["foeW", "nst"], ["a1"])
-        cp(T.ti[:], T.q0[:, 256:272], ["q0:t"], ["ti"])
-        op("V", lambda e: e.tensor_tensor(out=T.OD[:], in0=T.Dbuf[:].indirect(T.foeL[:]), in1=T.O[:], op=A.max), ["D", "D0", "foeL", "O0", "O1"], ["OD"])
         tt(mth, sw, nst, A.mult, ["q0:s", "nst"], ["mth"])
-        ts(T.ti2[:], T.ti[:], 1023, None, A.bitwise_and, None, ["ti"], ["ti2"])
-        tt(base, PW, a1, A.add, ["q3:W", "a1"], ["base"])
         tt(w6, sw, w7, A.mult, ["q0:s", "w7"], ["w6"])
-        cp(T.ZIu[:, 0:256:16], T.ti2[:], ["ti2"], ["ZIu"])
-        tt(foeW, FW, a1, A.add, ["q3:W", "a1"], ["foeW"])
         tt(wm, mth, base, A.mult, ["mth", "base"], ["wm"])
-        scan(T.uEs[:, 256 * t + 256:256 * t + 512], T.RST[:], T.ZIu[:], A.mult, A.add, ["RST", "ZIu"], ["uEs%d" % (t + 1)])
         tt(prevW, prevW, w6, A.add, ["prevW", "w6"], ["prevW"])
         tt(base2, base, wm, A.subtract, ["base", "wm"], ["base2"])
-        if not last:
-            v33(0, "q0:H", T.uEs, t + 1, "uEs%d" % (t + 1))
-            s1 = slice(256 * t + 256, 256 * t + 512)
-            send(to(t + 1), "aE%d" % (t + 1), T.uEl[:, s1], T.uEs[:, s1], "uEs%d" % (t + 1), "uEl%d" % (t + 1))
-            own_place(prevW, "prevW", T.Xps[:, s1], "Xps%d" % (t + 1))
-            send_prevs(t + 1)
-        else:
+        if last:
             for h in (0, 1):
                 mm(T.q0[:, half(h)], T.uEs[:, half(h, 256 * t + 256)], T.IDh[:], True, True, ["uEs%d" % (t + 1), "IDh"], ["q0:H"])
             act(T.OUT[:, 1024:1280], T.q0[:, 0:256], ["q0:H"], ["out4"])
@@ -486,33 +588,44 @@ def rank_program(g, core, T, topo):
                 output(x, k, 2 + i, T.U2[:, 256 * i:256 * i + 256], "U2:%d" % i)
             for i, y in ((4, T.yu), (2, T.yp), (3, T.yf)):
                 dma("Y", y[:], T.OUT[0:128:16, 256 * i:256 * i + 256], ["out%d" % i], [])
-        for h in (0, 1):
+        def names(h):
             p = 512 * t + 256 * h
             mm(XR[h][:, 0:128], T.BOh[:], T.PKl[:, p:p + 128], False, True, ["BOh", "PKl%d%d" % (t, h)], [("q4:X", "q2:X")[h]])
-        for h in (0, 1):
-            p = 512 * t + 256 * h
-            mm(T.q3[:, half(h, 256)], T.BOh[:], T.PKl[:, p + 128:p + 256], True, True, ["BOh", "PKl%d%d" % (t, h)], ["q3:n"])
-        for h in (0, 1):
-            tt(T.X1[:, half(h)], XR[h][:, 0:128], T.OD[:, half(h)], A.max, [("q4:X", "q2:X")[h], "OD"], ["X1"])
-            ts(T.O[:, half(h)], T.X1[:, half(h)], W - 1, None, A.bitwise_and, None, ["X1"], ["O%d" % h])
-            if not last:
-                look(h, T.PR, T.SH, T.offH, T.O, "O%d" % h, 0, "q0:H", "H")
-            else:
-                cp(T.OUT[:, half(h)], T.O[:, half(h)], ["O%d" % h], ["out0"])
-        if last:
-            dma("Y", T.yo[:], T.OUT[:, 0:256], ["out0"], [])
+            mm(T.q3[:, half(h, 256)], T.BOh[:], T.PKl[:, p + 128:p + 256], True, True, ["BOh", "PKl%d%d" % (t, h)], ["q3:n%d" % h])
+            tt(T.X1[:, half(h)], XR[h][:, 0:128], T.OD[:, half(h)], A.max, [("q4:X", "q2:X")[h], "OD"], ["X1%d" % h])
+            ts(T.O[:, half(h)], T.X1[:, half(h)], W - 1, None, A.bitwise_and, None, ["X1%d" % h], ["O%d" % h])
+
+        def new_targets(h):
+            tt(T.SM[:, half(h)], T.q3[:, half(h, 256)], T.MW[:, half(h)], A.mult, ["q3:n%d" % h, "MW"], ["SM"])
+            scan(T.EXp[:, half(h)], T.RST[:, half(h)], T.SM[:, half(h)], A.mult, A.add, ["RST", "SM"], ["EXp"])
+            if h == 1:
+                tt(nbm, T.EXp[:, 15:256:16], mth, A.mult, ["EXp", "mth"], ["nbm"])
+                tt(tauW, nbm, base2, A.add, ["nbm", "base2"], ["tauW"])
+
+        if not last:
+            names(0)
+            home_look(0)
+            home_gather(t + 1, 0)
+            new_targets(0)
+            home_gather(t + 1, 1)
+            names(1)
+            new_targets(1)
+            send_targets(t + 1)
+            home_look(1)
+            home_gather(t + 1, 2)
+            own_place(prevW, "prevW", T.Xps[:, s1], "Xps%d" % (t + 1))
+            send_prevs(t + 1)
         else:
-            home_gathers(t + 1, "S")
-        to_w(T.q3[:, 256:512], "q3:n", T.SM[:], "SM")
-        tt(nbm, T.EXp[:, 15:256:16], mth, A.mult, ["EXp", "mth"], ["nbm"])
-        tt(tauW, nbm, base2, A.add, ["nbm", "base2"], ["tauW"])
-        if last:
+            for h in (0, 1):
+                names(h)
+                new_targets(h)
+                cp(T.OUT[:, half(h)], T.O[:, half(h)], ["O%d" % h], ["out0"])
+            dma("Y", T.yo[:], T.OUT[:, 0:256], ["out0"], [])
             output(tauW, "tauW", 1, T.U2[:, 0:256], "U2:0")
             dma("S", T.yt[:], T.OUT[0:128:16, 256:512], ["out1"], [])
-        else:
-            send_targets(t + 1)
-            home_gathers(t + 1, "V")
 
+    for i in plan(prog):
+        issue(*prog[i][:5])
     for k in sorted(cnt):
         if cnt[k]:
             need("G", k, cnt[k])

@@ -1,10 +1,11 @@
+import numpy as np
 from concourse.mybir import AluOpType as A, ActivationFunctionType as F, AxisListType as AX
 
 N, RO, W = 8, 3, 2048
 LIFT, TOP, RHO = float(2 ** 48), float(2 ** 74), 2.25
 HCH = [[("S", 0, 64), ("S", 64, 128), ("S", 128, 208), ("V", 208, 256)],
-       [("S", 0, 88), ("V", 88, 128), ("S", 128, 216), ("V", 216, 256)]]
-OFF = [(1, 12)]
+       [("S", 0, 80), ("V", 80, 128), ("S", 128, 208), ("V", 208, 256)]]
+OFF = [(1, 12), (0, 12)]
 ENG = 16
 
 f32, bf, h16, i32, u16 = "float32", "bfloat16", "float16", "int32", "uint16"
@@ -54,7 +55,10 @@ TIME = {
           "X1": .11, "O": .11, "OHh": .21, "uEs1": .11, "uEs2": .11, "uEs3": .11, "PH": .14, "Q": .05, "E": .15, "out": .11},
     "S": {"": .2, "xH": 1.5, "xA": 2.6, "PTg": .38, "CTg": .38, "NBv": .38, "ZB": .42},
     "P": {"": .11, "K": .053, "q3:W": .053, "q0:t": .053, "q0:s": .053, "q0:g": .053, "U2": .11}, "G": {"": .5}}
-SELF, WAKE, HOP, LOAD = .2, .25, 3.0, 2.2
+SELF, WAKE, HOP, LOAD = 1, 2, 4, 3
+PLANNED = (0., .2, .25, 2.2, 2.4)
+CASES = ((1., (0., .15, .15, 2.2, 2.0), 1.0, 0, 75.), (1.2, (0., .15, .2, 2.2, 1.8), 1.2, 0, 90.), (1., (0., .2, .25, 2.5, 3.2), .9, 0, 80.))
+TURNS, PLANS = 1000, {}
 
 
 def cost(q, key):
@@ -63,17 +67,49 @@ def cost(q, key):
 
 def plan(prog):
     n = len(prog)
-    succ, npred = [[] for _ in range(n)], [0] * n
+    if n in PLANS:
+        return PLANS[n]
+    edges = links(prog)
+    rng = np.random.default_rng(1)
+    best, noise = None, np.ones(n)
+    for turn in range(TURNS):
+        new = noise * np.where(rng.random(n) < .01, 1 + .5 * rng.standard_normal(n), 1.) if turn else noise
+        order = greedy(prog, edges, [float(x) for x in new])
+        score = sum(length(prog, edges, order, case) / case[4] for case in CASES)
+        if best is None or score <= best[0]:
+            best, noise = (score, order), new
+    PLANS[n] = best[1]
+    return best[1]
+
+
+def length(prog, edges, order, case):
+    f, waits = case[0], case[1]
+    free, at = {q: 0. for q in "VSPGY"}, [0.] * len(prog)
+    end = 0.
+    for i in order:
+        q, c = prog[i][1], prog[i][5]
+        e = free[q] = max(free[q], at[i]) + (c if q in "GY" else c * f * (case[2] if c > .34 and q in "VS" else 1.))
+        for j, wait in edges[i]:
+            t = e + waits[wait]
+            if t > at[j]:
+                at[j] = t
+        end = max(end, e)
+    return end
+
+
+def links(prog):
+    n = len(prog)
+    succ = [[] for _ in range(n)]
     wr, rd, bank = {}, {}, {}
     for j, (kind, q, _, r, w, _c) in enumerate(prog):
         edge = {}
 
         def after(i, wait):
-            edge[i] = max(edge.get(i, 0.), wait)
+            edge[i] = max(edge.get(i, 0), wait)
 
         def result(i):
             ki, qi = prog[i][0], prog[i][1]
-            return HOP if ki == "send" else LOAD if ki == "dma" else (0. if q == "P" else SELF) if qi == q else WAKE
+            return HOP if ki == "send" else LOAD if ki == "dma" else (0 if q == "P" else SELF) if qi == q else WAKE
         for x in r:
             if x in wr:
                 after(wr[x], result(wr[x]))
@@ -90,7 +126,7 @@ def plan(prog):
                 for i in (runs[-2][1] if len(runs) > 1 else []):
                     after(i, WAKE)
                 if q == "P" and runs[-1][1]:
-                    after(runs[-1][1][-1], 0.)
+                    after(runs[-1][1][-1], 0)
                 runs[-1][1].append(j)
         for x in w:
             wr[x], rd[x] = j, []
@@ -99,10 +135,19 @@ def plan(prog):
         edge.pop(j, None)
         for i, wait in edge.items():
             succ[i].append((j, wait))
+    return succ
+
+
+def greedy(prog, succ, noise):
+    n, waits = len(prog), PLANNED
+    npred = [0] * n
+    for l in succ:
+        for j, _w in l:
             npred[j] += 1
     prio = [0.] * n
     for i in range(n - 1, -1, -1):
-        prio[i] = prog[i][5] + max([0.] + [wait + prio[j] for j, wait in succ[i]])
+        prio[i] = prog[i][5] + max([0.] + [waits[w] + prio[j] for j, w in succ[i]])
+    prio = [a * b for a, b in zip(prio, noise)]
     free = {q: 0. for q in "VSPGY"}
     ready = {q: [] for q in free}
     at, order = [0.] * n, []
@@ -123,7 +168,7 @@ def plan(prog):
         order.append(i)
         free[q] = start + prog[i][5]
         for j, wait in succ[i]:
-            at[j] = max(at[j], free[q] + wait)
+            at[j] = max(at[j], free[q] + waits[wait])
             npred[j] -= 1
             if npred[j] == 0:
                 ready[prog[j][1]].append(j)
@@ -520,6 +565,8 @@ def rank_program(g, core, T, topo):
         send(back(t), "aS%d" % t, SEl, SEs, "SEs%d" % t, "SEl%d" % t)
         score(0, 9, 11)
         tt(T.CS[:], T.q2[:, 256:512], SEs, A.mult, ["q2:D", "SEs%d" % t], ["CS"])
+        by_scalar(1)
+        add_scalar(1)
         score(0, 11, 16)
         open_keys(1)
         score(1, 0, 1)

import numpy as np
from concourse.mybir import AluOpType as A, ActivationFunctionType as F, AxisListType as AX

N, RO, W = 8, 3, 2048
LIFT, TOP, RHO = float(2 ** 48), float(2 ** 74), 2.25
HCH = [[("S", 0, 64), ("S", 64, 128), ("S", 128, 208), ("V", 208, 256)],
       [("S", 0, 80), ("V", 80, 128), ("S", 128, 208), ("V", 208, 256)]]
OFF = [(1, 12), (0, 12)]
ENG = 16

f32, bf, h16, i32, u16 = "float32", "bfloat16", "float16", "int32", "uint16"


def sb(n, d, p=128):
    return ("sbuf", [p, n], d)


SCRATCH = {
    "hue0": sb(W, bf), "hue1": sb(W, bf), "hue2": sb(W, bf),
    "O": sb(256, i32), "X1": sb(256, i32), "PR": sb(256, i32), "SH": sb(256, i32), "PA": sb(256, i32), "SA": sb(256, i32),
    "offH": sb(256, u16), "offA": sb(256, u16),
    "xH": sb(4096, bf), "xP": sb(4096, bf), "ZH": sb(4096, bf), "xA": sb(4096, bf), "ZA": sb(4096, bf), "ZB": sb(1024, bf), "cg": sb(16, bf), "ONE16": sb(128, bf),
    "Us": sb(768, bf), "Ul": sb(768, bf), "taus": sb(48, u16), "taul": sb(48, u16), "uEs": sb(1024, h16), "uEl": sb(768, h16),
    "Xps": sb(768, bf), "Xpl": sb(768, bf), "JOs": sb(768, h16), "JOl": sb(768, h16), "SEs": sb(768, bf), "SEl": sb(768, bf),
    "PKs": sb(1536, h16), "PKl": sb(1536, h16),
    "Nv": sb(256, f32), "NBv": sb(256, bf), "NB": sb(256, bf), "nbi": sb(256, i32),
    "PTg": sb(256, bf), "CTg": sb(256, bf), "PCT": sb(512, bf), "PTb": sb(256, bf),
    "gt": sb(256, bf), "okw": sb(256, bf), "CW": sb(256, bf), "PTx": sb(128, bf), "TabM": sb(256, bf),
    "Sc": sb(256, bf), "Ss": sb(256, bf), "ZIs": sb(256, bf), "ZIp": sb(256, bf), "ZIu": sb(256, h16), "EXp": sb(256, bf),
    "CS": sb(256, bf), "CP": sb(256, bf), "FPm": sb(256, bf), "SM": sb(256, bf), "PH": sb(256, f32), "Q": sb(272, f32),
    "E": sb(272, f32), "OHh": sb(256, bf), "OHa": sb(256, bf), "RQ": sb(272, bf), "Jenc": sb(256, bf),
    "NN": sb(256, f32), "Dbuf": sb(272, f32), "OD": sb(256, f32), "foeL": sb(16, u16), "ti": sb(16, i32), "ti2": sb(16, i32),
    "WS": sb(256, f32),
    "I8": sb(1024, i32, 8), "I8h": sb(1024, h16, 8), "RB": sb(128, h16, 8),
    "FI": sb(256, i32), "FL": sb(256, i32), "FH": sb(256, i32), "F7": sb(256, i32), "pi": sb(4, i32), "pf": sb(4, f32),
    "IDb": sb(128, bf), "IDn": sb(128, bf), "IDh": sb(128, h16), "ID2h": sb(128, h16), "ID8k": sb(128, bf), "C33": sb(128, h16),
    "BO2": sb(256, bf), "BOh": sb(128, h16), "BO8": sb(8, bf), "Bp": sb(8, bf), "MW": sb(256, bf), "IHI": sb(256, bf),
    "RST": sb(256, bf), "KB": sb(256, bf), "ONES": sb(128, bf), "wti": sb(1, i32), "wtf": sb(1, f32),
    "WT": sb(8, bf), "pw": sb(128, f32), "pw2": sb(128, f32), "cr": sb(128, f32), "cz": sb(128, f32),
    "wc": sb(2, f32), "w2c": sb(1, f32), "b1": sb(2, f32), "OUT": sb(1280, f32), "RX": sb(1408, bf),
}
BANKS = ("U2", "K1", "K2", "q0", "q1", "q2", "q3", "q4")
for _b in BANKS:
    SCRATCH[_b] = ("psum", [128, 512], f32)
PACKETS = ("aT", "aE", "aX", "aU", "aV", "aJ", "aS", "aP", "aR")
SEMAPHORES = (["sV", "sS", "sP", "sG", "loc"] + ["d%d" % k for k in range(20)]
              + [p + str(t) for p in PACKETS for t in range(RO)])


TIME = {
    "V": {"": .21, "pi": .05, "pf": .05, "RB": .11, "ID": .11, "C33": .05, "I8hpf": .42, "EXp": .08, "tauW": .05, "prevW": .05, "foeW": .05,
          "nst": .05, "a1": .05, "w": .05, "base": .05, "mth": .05, "nbm": .05, "taus": .05, "pr": .11, "sh": .11, "off": .11, "Bp": .05,
          "b1": .05, "wc0": .11, "w2c": .2, "ZIs": .05, "RX": .05, "xP": .45, "Us": .05, "xH": 1., "Nv": .37, "gt": .37, "ZA": .11,
          "okw": .11, "Ss": .11, "SEs": .11, "OHa": .11, "PKs": .11, "BO8": .05, "WT": .05, "ZI": .06, "ti": .05, "foeL": .05, "OD": .37,
          "X1": .11, "O": .11, "OHh": .21, "uEs1": .11, "uEs2": .11, "uEs3": .11, "PH": .14, "Q": .05, "E": .15, "out": .11},
    "S": {"": .2, "xH": 1.5, "xA": 2.6, "PTg": .38, "CTg": .38, "NBv": .38, "ZB": .42},
    "P": {"": .11, "K": .053, "q3:W": .053, "q0:t": .053, "q0:s": .053, "q0:g": .053, "U2": .11}, "G": {"": .5}}
SELF, WAKE, HOP, LOAD = 1, 2, 4, 3
PLANNED = (0., .2, .25, 2.2, 2.4)
CASES = ((1., (0., .15, .15, 2.2, 2.0), 1.0, 0, 75.), (1.2, (0., .15, .2, 2.2, 1.8), 1.2, 0, 90.), (1., (0., .2, .25, 2.5, 3.2), .9, 0, 80.))
TURNS, PLANS = 1000, {}


def cost(q, key):
    return TIME[q][max((k for k in TIME[q] if key.startswith(k)), key=len)] * 1.1


def plan(prog):
    n = len(prog)
    if n in PLANS:
        return PLANS[n]
    edges = links(prog)
    rng = np.random.default_rng(1)
    best, noise = None, np.ones(n)
    for turn in range(TURNS):
        new = noise * np.where(rng.random(n) < .01, 1 + .5 * rng.standard_normal(n), 1.) if turn else noise
        order = greedy(prog, edges, [float(x) for x in new])
        score = sum(length(prog, edges, order, case) / case[4] for case in CASES)
        if best is None or score <= best[0]:
            best, noise = (score, order), new
    PLANS[n] = best[1]
    return best[1]


def length(prog, edges, order, case):
    f, waits = case[0], case[1]
    free, at = {q: 0. for q in "VSPGY"}, [0.] * len(prog)
    end = 0.
    for i in order:
        q, c = prog[i][1], prog[i][5]
        e = free[q] = max(free[q], at[i]) + (c if q in "GY" else c * f * (case[2] if c > .34 and q in "VS" else 1.))
        for j, wait in edges[i]:
            t = e + waits[wait]
            if t > at[j]:
                at[j] = t
        end = max(end, e)
    return end


def links(prog):
    n = len(prog)
    succ = [[] for _ in range(n)]
    wr, rd, bank = {}, {}, {}
    for j, (kind, q, _, r, w, _c) in enumerate(prog):
        edge = {}

        def after(i, wait):
            edge[i] = max(edge.get(i, 0), wait)

        def result(i):
            ki, qi = prog[i][0], prog[i][1]
            return HOP if ki == "send" else LOAD if ki == "dma" else (0 if q == "P" else SELF) if qi == q else WAKE
        for x in r:
            if x in wr:
                after(wr[x], result(wr[x]))
        for x in w:
            if x in wr:
                after(wr[x], result(wr[x]))
            for i in rd.get(x, ()):
                after(i, SELF if prog[i][1] == q else WAKE)
        for b in {x.split(":")[0] for x in list(r) + list(w)}:
            if b in BANKS:
                runs = bank.setdefault(b, [])
                if not runs or runs[-1][0] != q:
                    runs.append((q, []))
                for i in (runs[-2][1] if len(runs) > 1 else []):
                    after(i, WAKE)
                if q == "P" and runs[-1][1]:
                    after(runs[-1][1][-1], 0)
                runs[-1][1].append(j)
        for x in w:
            wr[x], rd[x] = j, []
        for x in r:
            rd.setdefault(x, []).append(j)
        edge.pop(j, None)
        for i, wait in edge.items():
            succ[i].append((j, wait))
    return succ


def greedy(prog, succ, noise):
    n, waits = len(prog), PLANNED
    npred = [0] * n
    for l in succ:
        for j, _w in l:
            npred[j] += 1
    prio = [0.] * n
    for i in range(n - 1, -1, -1):
        prio[i] = prog[i][5] + max([0.] + [waits[w] + prio[j] for j, w in succ[i]])
    prio = [a * b for a, b in zip(prio, noise)]
    free = {q: 0. for q in "VSPGY"}
    ready = {q: [] for q in free}
    at, order = [0.] * n, []
    for i in range(n):
        if npred[i] == 0:
            ready[prog[i][1]].append(i)
    while len(order) < n:
        best = None
        for q, l in ready.items():
            if l:
                start = max(free[q], min(at[i] for i in l))
                i = max((i for i in l if at[i] <= start + .01), key=lambda i: (prio[i], -i))
                start = max(start, at[i])
                if best is None or start < best[0]:
                    best = (start, q, i)
        start, q, i = best
        ready[q].remove(i)
        order.append(i)
        free[q] = start + prog[i][5]
        for j, wait in succ[i]:
            at[j] = max(at[j], free[q] + waits[wait])
            npred[j] -= 1
            if npred[j] == 0:
                ready[prog[j][1]].append(j)
    return order


def rank_program(g, core, T, topo):
    rank = T.rank_of(core)
    if rank is None:
        return
    tauW, prevW, foeW, nst, a1, w6, w7, base, mth, base2, nbm, wm = [T.WS[:, 16 * i:16 * i + 16] for i in range(12)]
    q_of = {"V": g.vector, "S": g.scalar, "P": g.tensor, "G": g, "Y": g.sync}
    cnt = {"sV": 0, "sS": 0, "sP": 0, "sG": 0, "loc": 0}
    known = {k: {} for k in q_of}
    snap = {}
    wr, rd, bank, ndma = {}, {}, {}, [0]

    def need(q, sem, val):
        k = known[q]
        if k.get(sem, 0) >= val:
            return
        q_of[q].wait_ge(T.sem[sem], val)
        k[sem] = val
        for s, v in snap.get((sem, val), {}).items():
            k[s] = max(k.get(s, 0), v)

    def deps(q, r, w, me):
        todo = {}

        def add(s, v):
            todo[s] = max(todo.get(s, 0), v)
        for x in r:
            if x in wr:
                add(*wr[x])
        for x in w:
            if x in wr and not (me == "sP" and wr[x][0] == "sP"):
                add(*wr[x])
            for s, v in rd.get(x, {}).items():
                add(s, v)
        for x in list(r) + list(w):
            b = x.split(":")[0]
            if b in BANKS:
                for s, v in bank.get(b, {}).items():
                    if s != me:
                        add(s, v)
        for s in sorted(todo, key=lambda s: -todo[s]):
            need(q, s, todo[s])

    def note(r, w, sem, val):
        for x in w:
            wr[x] = (sem, val)
            rd[x] = {}
        for x in r:
            rd.setdefault(x, {})[sem] = val
        for x in list(r) + list(w):
            b = x.split(":")[0]
            if b in BANKS:
                bank.setdefault(b, {})[sem] = val

    prog = []

    def op(q, call, r, w):
        prog.append(("op", q, call, r, w, cost(q, w[0])))

    def dma(q, out, in_, r, w):
        prog.append(("dma", q, (out, in_), r, w, 0.1))

    def send(dst, arr, out, in_, src, land):
        prog.append(("send", "G", (dst, arr, out, in_), [src], [land], 1.0))

    def issue(kind, q, what, r, w):
        if kind == "op":
            sem = "s" + q
            deps(q, r, w, sem)
            cnt[sem] += 1
            snap[(sem, cnt[sem])] = dict(known[q])
            what(q_of[q]).then_inc(T.sem[sem], 1)
            note(r, w, sem, cnt[sem])
        elif kind == "dma":
            sem = "d%d" % ndma[0]
            ndma[0] += 1
            deps(q, r, w, "")
            snap[(sem, 16)] = dict(known[q])
            q_of[q].dma_start(*what).then_inc(T.sem[sem], 16)
            note(r, w, sem, 16)
        else:
            dst, arr, out, in_ = what
            deps("G", r, [], "")
            rid, pid = topo.addr(dst)[:2]
            eng = topo.engines(core, dst)[:ENG]
            g.remote_dma(out, in_, T.sem[arr], T.sem.loc, pid, rid, sum(1 << e for e in eng))
            cnt["loc"] += len(eng)
            wr[w[0]] = (arr, len(eng))
            rd[w[0]] = {}

    def tt(out, a, b, o, r, w):
        op("V", lambda e: e.tensor_tensor(out=out, in0=a, in1=b, op=o), r, w)

    def ts(out, a, s1, s2, o0, o1, r, w):
        if o1 is None:
            op("V", lambda e: e.tensor_scalar(out=out, in0=a, scalar1=s1, scalar2=None, op0=o0), r, w)
        else:
            op("V", lambda e: e.tensor_scalar(out=out, in0=a, scalar1=s1, scalar2=s2, op0=o0, op1=o1), r, w)

    def cp(out, a, r, w):
        op("V", lambda e: e.tensor_copy(out=out, in_=a), r, w)

    def scan(out, d0, d1, o0, o1, r, w, init=0.0):
        op("V", lambda e: e.tensor_tensor_scan(out=out, data0=d0, data1=d1, initial=init, op0=o0, op1=o1), r, w)

    def act(out, a, r, w, fn=None, **kw):
        op("S", lambda e: e.activation(out=out, in_=a, func=fn or F.Copy, **kw), r, w)

    def mm(out, l, rh, start, stop, r, w):
        op("P", lambda e: e.matmul(out=out, lhsT=l, rhs=rh, start=start, stop=stop), r, w)

    def fill(out, c, w):
        op("V", lambda e: e.memset(out, c), [], w)

    def half(h, at=0):
        return slice(at + 128 * h, at + 128 * h + 128)

    def to(t):
        return T.cores[(rank + 1 + t) % N]

    def back(t):
        return T.cores[(rank - 1 - t) % N]

    dma("Y", T.I8[:, 768:1024], T.tas[:], [], ["I8u"])
    dma("S", T.I8[:, 0:256], T.tau[:], [], ["I8t"])
    dma("Y", T.O[:], T.own[:], [], ["O0", "O1"])
    dma("S", T.I8[:, 256:512], T.prev[:], [], ["I8p"])
    dma("Y", T.hue0[:], T.hue[:], [], ["hue0"])
    dma("S", T.I8[:, 512:768], T.foe[:], [], ["I8f"])
    dma("Y", T.nbi[:], T.nb[:], [], ["nbi"])
    dma("Y", T.wti[:], T.wt[:], [], ["wti"])
    for t in (1, 2):
        hb, s = T["hue%d" % t], 77 * t
        dma("Y", hb[:, 0:W - s], T.hue[:, s:W], [], ["hue%da" % t])
        dma("Y", hb[:, W - s:W], T.hue[:, 0:s], [], ["hue%db" % t])

    op("G", lambda e: e.iota(T.pi[:, 0:1], [[0, 1]], 0, 1), [], ["pi0"])
    op("G", lambda e: e.iota(T.FI[:], [[1, 256]], 0, 0), [], ["FI"])
    op("G", lambda e: e.iota(T.KB[:], [[0, 16], [-1, 16]], 15, 0, allow_small_or_imprecise_dtypes=True), [], ["KB"])
    ts(T.pi[:, 1:2], T.pi[:, 0:1], 15, None, A.bitwise_and, None, ["pi0"], ["pi1"])
    ts(T.pi[:, 2:3], T.pi[:, 0:1], 4, None, A.arith_shift_right, None, ["pi0"], ["pi2"])
    cp(T.pf[:, 0:3], T.pi[:, 0:3], ["pi0", "pi1", "pi2"], ["pf"])
    p0, pl, pg = T.pf[:, 0:1], T.pf[:, 1:2], T.pf[:, 2:3]
    ts(T.FH[:], T.FI[:], 4, None, A.arith_shift_right, None, ["FI"], ["FH"])
    ts(T.RB[:], T.FH[0:8, 0:128], T.pf[0:8, 0:1], None, A.is_equal, None, ["FH", "pf"], ["RB"])
    ts(T.FL[:], T.FI[:], 15, None, A.bitwise_and, None, ["FI"], ["FL"])
    ts(T.IDh[:], T.FI[:, 0:128], p0, None, A.is_equal, None, ["FI", "pf"], ["IDh"])
    ts(T.ID2h[:], T.IDh[:], 2.0, None, A.mult, None, ["IDh"], ["ID2h"])
    ts(T.C33[:], T.IDh[:], 0.0, 33.0, A.mult, A.add, ["IDh"], ["C33"])
    cp(T.I8h[:, 768:1024], T.I8[:, 768:1024], ["I8u"], ["I8hu"])
    for h in (0, 1):
        mm(T.q1[:, half(h)], T.I8h[:, half(h, 768)], T.RB[:], True, True, ["I8hu", "RB"], ["q1:u"])
    ts(T.I8h[:, 0:256], T.I8[:, 0:256], 1.0, None, A.add, None, ["I8t"], ["I8ht"])
    mm(T.q2[:, 0:256], T.RB[:], T.I8h[:, 0:256], True, True, ["I8ht", "RB"], ["q2:t"])
    cp(T.uEs[:, 0:256], T.q1[:, 0:256], ["q1:u"], ["uEs0"])

    def v33(reg, key, src, t, ukey):
        for h in (0, 1):
            mm(T.q0[:, half(h, reg)], T.IDh[:], T.C33[:], True, False, ["IDh", "C33"], [key])
            mm(T.q0[:, half(h, reg)], src[:, half(h, 256 * t)], T.ID2h[:], False, True, [ukey, "ID2h"], [key])

    v33(0, "q0:H", T.uEs, 0, "uEs0")
    send(to(0), "aE0", T.uEl[:, 0:256], T.uEs[:, 0:256], "uEs0", "uEl0")
    ts(T.MW[:], T.FL[:], pl, None, A.is_equal, None, ["FL", "pf"], ["MW"])
    ts(T.RST[:], T.FL[:], 0.5, None, A.is_gt, None, ["FL"], ["RST"])

    def to_w(wide, wkey, tile, tkey):
        tt(tile, wide, T.MW[:], A.mult, [wkey, "MW"], [tkey])
        scan(T.EXp[:], T.RST[:], tile, A.mult, A.add, ["RST", tkey], ["EXp"])

    def send_targets(t):
        o = slice(16 * t, 16 * t + 16)
        ts(T.taus[:, o], tauW, -1.0, None, A.add, None, ["tauW"], ["taus%d" % t])
        send(to(t), "aT%d" % t, T.taul[:, o], T.taus[:, o], "taus%d" % t, "taul%d" % t)

    to_w(T.q2[:, 0:256], "q2:t", T.SM[:], "SM")
    cp(tauW, T.EXp[:, 15:256:16], ["EXp"], ["tauW"])
    send_targets(0)

    def look(h, pr, sh, off, o, okey, vreg, vkey, tag):
        b = half(h)
        tt(pr[:, b], o[:, b], T.q0[:, half(h, vreg)], A.mult, [okey, vkey], ["pr%s%d" % (tag, h)])
        ts(sh[:, b], pr[:, b], 5, W - 1, A.arith_shift_right, A.bitwise_and, ["pr%s%d" % (tag, h)], ["sh%s%d" % (tag, h)])
        cp(off[:, b], sh[:, b], ["sh%s%d" % (tag, h)], ["off%s%d" % (tag, h)])

    def gather(e, t, buf, off, tag, i, c0, c1):
        src = T["hue%d" % t][:, 0:W].indirect(off[:, c0:c1])
        r = ["off%s%d" % (tag, h) for h in (0, 1) if c0 < 128 * h + 128 and c1 > 128 * h]
        r += ["hue0"] if t == 0 else ["hue%da" % t, "hue%db" % t]
        if e == "S":
            act(buf[:, 16 * c0:16 * c1], src, r, ["x%s%d" % (tag, i)])
        else:
            cp(buf[:, 16 * c0:16 * c1], src, r, ["x%s%d" % (tag, i)])

    def home_gather(t, i):
        gather(HCH[min(t, 1)][i][0], t, T.xH, T.offH, "H", i, *HCH[min(t, 1)][i][1:])

    def home_look(h):
        look(h, T.PR, T.SH, T.offH, T.O, "O%d" % h, 0, "q0:H", "H")

    def home_best(t, h):
        for i in (2 * h, 2 * h + 1):
            c0, c1 = HCH[min(t, 1)][i][1:]
            scan(T.xP[:, 16 * c0:16 * c1], T.RX[:, 0:16 * (c1 - c0)], T.xH[:, 16 * c0:16 * c1], A.mult, A.max, ["RX", "xH%d" % i], ["xP%d" % i])
        b = half(h, 256 * t)
        cp(T.Us[:, b], T.xP[:, 2048 * h + 15:2048 * h + 2048:16], ["xP%d" % (2 * h), "xP%d" % (2 * h + 1)], ["Us%d%d" % (t, h)])
        send(to(t), "aUaV"[2 * h:2 * h + 2] + str(t), T.Ul[:, b], T.Us[:, b], "Us%d%d" % (t, h), "Ul%d%d" % (t, h))

    def const(out, shape, key, c):
        act(out, shape, ["KB"], [key], scale=0.0, bias=c)

    for i in range(0, 1408, 256):
        j = min(i + 256, 1408)
        const(T.RX[:, i:j], T.KB[:, 0:j - i], "RX", 1.0)
    const(T.cr[:], T.KB[:, 0:128], "cr", 1.0 / RHO)
    const(T.cz[:], T.KB[:, 0:128], "cz", 0.0)
    for h in (0, 1):
        home_look(h)
    for i in (0, 1, 2):
        home_gather(0, i)

    ts(T.IHI[:], T.FH[:], pl, None, A.is_equal, None, ["FH", "pf"], ["IHI"])
    ts(T.I8h[:, 256:768], T.I8[:, 256:768], 1.0, None, A.add, None, ["I8p", "I8f"], ["I8hpf"])
    mm(T.q3[:], T.RB[:], T.I8h[:, 256:768], True, True, ["I8hpf", "RB"], ["q3:w"])
    to_w(T.q3[:, 256:512], "q3:w", T.SM[:], "SM")
    cp(foeW, T.EXp[:, 15:256:16], ["EXp"], ["foeW"])
    to_w(T.q3[:, 0:256], "q3:w", T.Xps[:, 0:256], "Xps0")
    cp(prevW, T.EXp[:, 15:256:16], ["EXp"], ["prevW"])

    def send_prevs(t):
        s = slice(256 * t, 256 * t + 256)
        send(to(t), "aX%d" % t, T.Xpl[:, s], T.Xps[:, s], "Xps%d" % t, "Xpl%d" % t)

    send_prevs(0)
    ts(T.IDb[:], T.FI[:, 0:128], p0, None, A.is_equal, None, ["FI", "pf"], ["IDb"])
    ts(T.Bp[:], T.FI[:, 0:8], pg, 16.0, A.is_equal, A.mult, ["FI", "pf"], ["Bp"])
    ts(T.F7[:], T.FH[:], 7, None, A.bitwise_and, None, ["FH"], ["F7"])
    ts(T.BO2[:], T.F7[:], pg, None, A.is_equal, None, ["F7", "pf"], ["BO2"])
    ts(T.b1[:, 0:1], p0, 1.0, None, A.add, None, ["pf"], ["b10"])
    ts(T.b1[:, 1:2], p0, 129.0, None, A.add, None, ["pf"], ["b11"])
    ts(T.NB[:], T.nbi[:], 1.0, None, A.add, None, ["nbi"], ["NB"])
    ts(T.RQ[:, 0:256], T.FL[:], 14.5, None, A.is_lt, None, ["FL"], ["RQ0"])
    ts(T.RQ[:, 256:272], T.FL[:, 0:16], 14.5, None, A.is_lt, None, ["FL"], ["RQ1"])
    fill(T.Q[:], 0.0, ["Q0", "Q1"])
    scan(T.pw[:], T.cr[:], T.cz[:], A.mult, A.add, ["cr", "cz"], ["pw"], init=TOP)
    tt(T.pw2[:], T.pw[:], T.IDb[:], A.mult, ["pw", "IDb"], ["pw2"])
    op("V", lambda e: e.tensor_reduce(out=T.wc[:, 0:1], in_=T.pw2[:], axis=AX.X, op=A.add), ["pw2"], ["wc0"])
    ts(T.wc[:, 1:2], T.wc[:, 0:1], 1 / LIFT, None, A.mult, None, ["wc0"], ["wc1"])
    op("V", lambda e: e.reciprocal(out=T.w2c[:, 0:1], in_=T.wc[:, 0:1]), ["wc0"], ["w2c"])
    ts(T.w2c[:, 0:1], T.w2c[:, 0:1], LIFT, None, A.mult, None, ["w2c"], ["wx"])
    fill(T.ZIs[:], 0.0, ["ZIs"])
    fill(T.RX[:, 0:1408:16], 0.0, ["RX"])
    const(T.ONES[:], T.KB[:, 0:128], "ONES", 1.0)
    const(T.ONE16[:], T.KB[:, 0:128], "ONE16", 1.0 / 16)
    act(T.IDn[:], T.IDb[:], ["IDb"], ["IDn"], scale=-1.0)
    act(T.ID8k[:], T.IDb[:], ["IDb"], ["ID8k"], scale=8192.0)

    def later_constants():
        ts(T.BOh[:], T.F7[:, 0:128], pg, None, A.is_equal, None, ["F7", "pf"], ["BOh"])
        ts(T.BO8[:], T.FI[:, 0:8], pg, None, A.is_equal, None, ["FI", "pf"], ["BO8"])
        cp(T.wtf[:], T.wti[:], ["wti"], ["wtf"])
        ts(T.WT[:], T.BO8[:], T.wtf[:, 0:1], None, A.mult, None, ["BO8", "wtf"], ["WT"])
        fill(T.Dbuf[:], 0.0, ["D", "D0"])
        fill(T.ZIp[:], 0.0, ["ZIp"])
        cp(T.ZIu[:], T.ZIp[:], ["ZIp"], ["ZIu"])
        cp(T.K2[:, 128:384], T.MW[:], ["MW"], ["K2:M"])

    def pick(kap, kkey, c0, c1, oh, okey):
        hs = range(c0 // 128, c1 // 128)
        kp, kq = ["PH%d" % h for h in hs], ["Q%d" % h for h in hs]
        scan(T.PH[:, c0:c1], T.RST[:, c0:c1], kap, A.mult, A.max, ["RST", kkey], kp)
        cp(T.Q[:, c0 + 15:c1:16], T.PH[:, c0 + 15:c1:16], kp, kq)
        scan(T.E[:, c0:c1 + 15], T.RQ[:, c0:c1 + 15], T.Q[:, c0:c1 + 15], A.mult, A.add, ["RQ0", "RQ1"] + kq, ["E0", "E1"])
        tt(oh[:, c0:c1], T.E[:, c0 + 15:c1 + 15], kap, A.is_equal, ["E0", "E1", kkey], [okey])

    def own_place(x, k, tile, tkey):
        cp(T.ZIp[:, 0:256:16], x, [k], ["ZIp"])
        scan(T.EXp[:], T.RST[:], T.ZIp[:], A.mult, A.add, ["RST", "ZIp"], ["EXp"])
        tt(tile, T.EXp[:], T.K2[:, 128:384], A.mult, ["EXp", "K2:M"], [tkey])

    def output(x, k, i, ps, pk):
        own_place(x, k, T.SM[:], "SM")
        mm(ps, T.BO2[:, 0:128], T.SM[:], True, True, ["BO2", "SM"], [pk])
        act(T.OUT[:, 256 * i:256 * i + 256], ps, [pk], ["out%d" % i], F.Identity, bias=-1.0)

    for t in range(RO):
        s = slice(256 * t, 256 * t + 256)
        last = t == RO - 1
        Us, Ul, SEs, SEl, tau = T.Us[:, s], T.Ul[:, s], T.SEs[:, s], T.SEl[:, s], T.taul[:, 16 * t:16 * t + 16]
        tl = "taul%d" % t
        kUs, kUl = ["Us%d0" % t, "Us%d1" % t], ["Ul%d0" % t, "Ul%d1" % t]
        home_best(t, 0)
        home_gather(t, 3)
        home_best(t, 1)
        v33(256, "q0:A", T.uEl, t, "uEl%d" % t)
        cp(T.Nv[:], T.O[:].indirect(tau), ["O0", "O1", tl], ["Nv"])
        for h in (0, 1):
            look(h, T.PA, T.SA, T.offA, T.Nv, "Nv", 256, "q0:A", "A")
        act(T.PTg[:], T.MW[:].indirect(tau), ["MW", tl], ["PTg"])
        act(T.CTg[:], T.IHI[:].indirect(tau), ["IHI", tl], ["CTg"])
        gather("S", t, T.xA, T.offA, "A", 0, 0, 128)
        for h in (0, 1):
            mm(T.q2[:, half(h)], T.PTg[:, half(h)], T.IDb[:], True, True, ["PTg", "IDb"], ["q2:D"])
            mm(T.q2[:, half(h, 256)], T.CTg[:, half(h)], T.IDb[:], True, True, ["CTg", "IDb"], ["q2:D"])
        act(T.PCT[:, 0:256], T.q2[:, 0:256], ["q2:D"], ["PT"])
        act(T.PCT[:, 256:512], T.q2[:, 256:512], ["q2:D"], ["CT"], scale=1 / 2.02)
        act(T.PTx[:], T.q2[:, 0:128], ["q2:D", "wx"], ["PTx"], scale=T.w2c[:, 0:1])
        for h in (0, 1):
            act(T.PTb[:, half(h)], T.q2[:, half(h)], ["q2:D", "b1%d" % h], ["PTb%d" % h], scale=T.b1[:, h:h + 1])
        gather("S", t, T.xA, T.offA, "A", 1, 128, 256)
        mm(T.U2[:, 0:256], T.IDb[:], Us, True, True, ["IDb"] + kUs, ["U2:H"])
        mm(T.K1[:, 0:256], T.IDb[:], T.KB[:], True, False, ["IDb", "KB"], ["K1:H"])
        for k in range(16):
            tt(T.ZH[:, 256 * k:256 * k + 256], T.xH[:, k:4096:16], T.U2[:, 0:256], A.not_equal, ["xH0", "xH1", "xH2", "xH3", "U2:H"], ["ZH%d" % k])
            for h in (0, 1):
                mm(T.K1[:, 128 * h + k:128 * h + 128:16], T.ZH[:, half(h, 256 * k)], T.Bp[:], False, (k, h) == (15, 1), ["ZH%d" % k, "Bp"], ["K1:H"])
        KA = (T.K2, T.K1)
        kk = ("K2:A", "K1:A")
        kA = (["xA0"], ["xA1"])
        mine = {h: [k for k in range(16) if not any(o == h and f <= k < f + 4 for o, f in OFF)] for h in (0, 1)}

        def by_scalar(i):
            h, f = OFF[i]
            for j in range(4):
                mm(T.q0[:, half(j)], T.IDb[:], T.xA[:, 2048 * h + f + j:2048 * h + 2048:16], True, False, ["IDb"] + kA[h], ["q0:d"])
                mm(T.q0[:, half(j)], T.IDn[:], T.Ul[:, half(h, 256 * t)], False, True, ["IDn", kUl[h]], ["q0:d"])
            act(T.ZB[:, 512 * i:512 * i + 512], T.q0[:], ["q0:d"], ["ZB%d" % i], F.Relu)

        def open_keys(h):
            mm(KA[h][:, 0:128], T.IDb[:], T.KB[:, 0:128], True, False, ["IDb", "KB"], [kk[h]])

        def add_scalar(i):
            h, f = OFF[i]
            for j in range(4):
                k = f + j
                mm(KA[h][:, k:128:16], T.Ul[:, half(h, 256 * t)], T.Bp[:], False, False, [kUl[h], "Bp"], [kk[h]])
                mm(KA[h][:, k:128:16], T.ZB[:, half(j, 512 * i)], T.Bp[:], False, False, ["ZB%d" % i, "Bp"], [kk[h]])

        def score(h, a, b):
            for k in mine[h][a:b]:
                z = T.ZA[:, half(h, 256 * k)]
                tt(z, T.xA[:, 2048 * h + k:2048 * h + 2048:16], T.U2[:, half(h, 256)], A.max, kA[h] + ["U2:A%d" % h], ["ZA%d_%d" % (h, k)])
                mm(KA[h][:, k:128:16], z, T.Bp[:], False, k == mine[h][-1], ["ZA%d_%d" % (h, k), "Bp"], [kk[h]])

        def best(h):
            pick(KA[h][:, 0:128], kk[h], 128 * h, 128 * h + 128, T.OHa, "OHa%d" % h)
            mm(T.q1[:, half(h)], T.OHa[:, half(h)], T.IDb[:], True, True, ["OHa%d" % h, "IDb"], ["q1:o"])

        def loot(h):
            p = 512 * t + 256 * h
            tt(T.PKs[:, p:p + 128], T.q1[:, half(h)], T.Nv[:, half(h)], A.mult, ["q1:o", "Nv"], ["PKs%d%d" % (t, h)])
            tt(T.PKs[:, p + 128:p + 256], T.q1[:, half(h)], T.NBv[:, half(h)], A.mult, ["q1:o", "NBv"], ["PKs%d%d" % (t, h)])
            send(back(t), "aPaR"[2 * h:2 * h + 2] + str(t), T.PKl[:, p:p + 256], T.PKs[:, p:p + 256], "PKs%d%d" % (t, h), "PKl%d%d" % (t, h))

        for h in (0, 1):
            mm(T.U2[:, half(h, 256)], T.IDb[:], T.Ul[:, half(h, 256 * t)], True, True, ["IDb", kUl[h]], ["U2:A%d" % h])
        tt(T.gt[:], Us.indirect(tau), Ul, A.is_gt, kUs + kUl + [tl], ["gt"])
        for h in (0, 1):
            mm(T.q3[:, half(h, 256)], T.Xpl[:, half(h, 256 * t)], T.BO2[:, 0:128], True, True, ["Xpl%d" % t, "BO2"], ["q3:p"])
        for h in (0, 1):
            mm(T.q3[:, half(h)], T.gt[:, half(h)], T.BO2[:, 0:128], True, True, ["gt", "BO2"], ["q3:c"])
        pick(T.K1[:, 0:256], "K1:H", 0, 256, T.OHh, "OHh")
        for h in (0, 1):
            mm(T.q1[:, half(h)], T.OHh[:, half(h)], T.IDb[:], True, True, ["OHh", "IDb"], ["q1:o"])
        for h in (0, 1):
            ts(T.okw[:, half(h)], T.q3[:, half(h)], 7.5, T.wc[:, h:h + 1], A.is_lt, A.mult, ["q3:c", "wc%d" % h], ["okw"])
        tt(T.CW[:], T.q2[:, 256:512], T.okw[:], A.mult, ["q2:D", "okw"], ["CW"])
        mm(T.q4[:, 0:128], T.PCT[:, 0:128], T.CW[:, 0:128], True, True, ["PT", "CW"], ["q4:T"])
        mm(T.q4[:, 128:256], T.PTx[:], T.CW[:, 0:128], True, False, ["PTx", "CW"], ["q4:T"])
        mm(T.q4[:, 128:256], T.PCT[:, 128:256], T.CW[:, 128:256], False, True, ["PT", "CW"], ["q4:T"])
        tt(T.JOs[:, s], T.q1[:, 0:256], T.O[:], A.mult, ["q1:o", "O0", "O1"], ["JOs%d" % t])
        send(to(t), "aJ%d" % t, T.JOl[:, s], T.JOs[:, s], "JOs%d" % t, "JOl%d" % t)
        act(T.Jenc[:], T.q1[:, 0:256], ["q1:o"], ["Jenc"], scale=12288.0, bias=-16384.0)
        act(T.NBv[:], T.NB[:].indirect(tau), ["NB", tl], ["NBv"])
        open_keys(0)
        score(0, 0, 3)
        tt(T.TabM[:], T.q4[:, 0:256], T.BO2[:], A.mult, ["q4:T", "BO2"], ["TabM"])
        for h in (0, 1):
            mm(T.q4[:, half(h, 256)], T.PTg[:, half(h)], T.TabM[:, half(h)], True, True, ["PTg", "TabM"], ["q4:S"])
        score(0, 3, 6)
        tt(T.Sc[:], T.q4[:, 256:512], T.PCT[:, 256:512], A.mult, ["q4:S", "CT"], ["Sc"])
        score(0, 6, 7)
        by_scalar(0)
        scan(T.Ss[:], T.RST[:], T.Sc[:], A.mult, A.add, ["RST", "Sc"], ["Ss"])
        score(0, 7, 8)
        tt(T.ZIs[:, 0:256:16], T.Ss[:, 15:256:16], T.okw[:, 0:256:16], A.is_lt, ["Ss", "okw"], ["ZIs"])
        score(0, 8, 9)
        scan(SEs, T.RST[:], T.ZIs[:], A.mult, A.add, ["RST", "ZIs"], ["SEs%d" % t])
        send(back(t), "aS%d" % t, SEl, SEs, "SEs%d" % t, "SEl%d" % t)
        score(0, 9, 11)
        tt(T.CS[:], T.q2[:, 256:512], SEs, A.mult, ["q2:D", "SEs%d" % t], ["CS"])
        by_scalar(1)
        add_scalar(1)
        score(0, 11, 16)
        open_keys(1)
        score(1, 0, 1)
        tt(T.CP[:], T.q3[:, 256:512], T.CS[:], A.mult, ["q3:p", "CS"], ["CP"])
        best(0)
        for h in (0, 1):
            mm(T.q3[:, 0:128], T.PTb[:, half(h)], T.CS[:, half(h)], h == 0, h == 1, ["PTb%d" % h, "CS"], ["q3:F"])
        for h in (0, 1):
            mm(T.q3[:, 128:256], T.PCT[:, half(h)], T.CP[:, half(h)], h == 0, h == 1, ["PT", "CP"], ["q3:F"])
        score(1, 1, 3)
        loot(0)
        if t == 0:
            later_constants()
        tt(T.FPm[:], T.q3[:, 0:256], T.BO2[:], A.mult, ["q3:F", "BO2"], ["FPm"])
        add_scalar(0)
        score(1, 3, 16)
        best(1)
        for h in (0, 1):
            mm(T.q0[:, 288:304], T.SEs[:, half(h, 256 * t)], T.ONES[:, 0:16], h == 0, h == 1, ["SEs%d" % t, "ONES"], ["q0:g"])
        act(T.cg[:], T.q0[:, 288:304], ["q0:g"], ["cg"])
        mm(T.q0[:, 256:272], T.ONE16[:], T.cg[:], True, False, ["ONE16", "cg"], ["q0:t"])
        for h in (0, 1):
            mm(T.q0[:, 256 + 8 * h:264 + 8 * h], T.Us[:, half(h, 256 * t)], T.WT[:], False, h == 1, [kUs[h], "WT"], ["q0:t"])
        for x in (0, 1):
            for gg in range(8):
                mm(T.q3[:, 256 + 16 * x:272 + 16 * x], T.IDb[:], T.FPm[:, 128 * x + 16 * gg:128 * x + 16 * gg + 16], gg == 0, gg == 7,
                   ["IDb", "FPm"], ["q3:W"])
        loot(1)
        mm(T.q1[:, 256:512], T.BOh[:], T.JOl[:, s], True, True, ["BOh", "JOl%d" % t], ["q1:n"])
        act(T.NN[:], T.q1[:, 256:512], ["q1:n"], ["NN"], F.Identity, bias=8192.0)
        cp(T.ti[:], T.q0[:, 256:272], ["q0:t"], ["ti"])
        ts(T.ti2[:], T.ti[:], 1023, None, A.bitwise_and, None, ["ti"], ["ti2"])
        cp(T.ZIu[:, 0:256:16], T.ti2[:], ["ti2"], ["ZIu"])
        scan(T.uEs[:, 256 * t + 256:256 * t + 512], T.RST[:], T.ZIu[:], A.mult, A.add, ["RST", "ZIu"], ["uEs%d" % (t + 1)])
        s1 = slice(256 * t + 256, 256 * t + 512)
        if not last:
            v33(0, "q0:H", T.uEs, t + 1, "uEs%d" % (t + 1))
            send(to(t + 1), "aE%d" % (t + 1), T.uEl[:, s1], T.uEs[:, s1], "uEs%d" % (t + 1), "uEl%d" % (t + 1))

        FW, PW, FPW, sw = T.q3[:, 256:272], T.q3[:, 272:288], T.q3[:, 256:288], T.q0[:, 272:288]
        cp(T.foeL[:], FW, ["q3:W"], ["foeL"])
        ts(nst, FW, 0.5, None, A.is_lt, None, ["q3:W"], ["nst"])
        tt(w7, tauW, prevW, A.subtract, ["tauW", "prevW"], ["w7"])
        tt(T.Dbuf[:, 1:257], T.q1[:, 0:256], T.NN[:], A.mult, ["q1:o", "NN"], ["D"])
        tt(a1, foeW, nst, A.mult, ["foeW", "nst"], ["a1"])
        op("V", lambda e: e.tensor_tensor(out=T.OD[:], in0=T.Dbuf[:].indirect(T.foeL[:]), in1=T.O[:], op=A.max), ["D", "D0", "foeL", "O0", "O1"], ["OD"])
        tt(base, PW, a1, A.add, ["q3:W", "a1"], ["base"])
        tt(foeW, FW, a1, A.add, ["q3:W", "a1"], ["foeW"])
        tt(T.SM[:], SEl, T.K2[:, 128:384], A.mult, ["SEl%d" % t, "K2:M"], ["SM"])
        XR = (T.q4, T.q2)
        for h in (0, 1):
            mm(XR[h][:, 0:128], T.IDb[:], T.Jenc[:, half(h)], True, False, ["IDb", "Jenc"], [("q4:X", "q2:X")[h]])
            mm(XR[h][:, 0:128], T.SEl[:, half(h, 256 * t)], T.ID8k[:], False, False, ["SEl%d" % t, "ID8k"], [("q4:X", "q2:X")[h]])
        for h in (0, 1):
            mm(T.q0[:, 272 + 8 * h:280 + 8 * h], T.SM[:, half(h)], T.BO8[:], True, True, ["SM", "BO8"], ["q0:s"])
        tt(mth, sw, nst, A.mult, ["q0:s", "nst"], ["mth"])
        tt(w6, sw, w7, A.mult, ["q0:s", "w7"], ["w6"])
        tt(wm, mth, base, A.mult, ["mth", "base"], ["wm"])
        tt(prevW, prevW, w6, A.add, ["prevW", "w6"], ["prevW"])
        tt(base2, base, wm, A.subtract, ["base", "wm"], ["base2"])
        if last:
            for h in (0, 1):
                mm(T.q0[:, half(h)], T.uEs[:, half(h, 256 * t + 256)], T.IDh[:], True, True, ["uEs%d" % (t + 1), "IDh"], ["q0:H"])
            act(T.OUT[:, 1024:1280], T.q0[:, 0:256], ["q0:H"], ["out4"])
            for i, (x, k) in enumerate(((prevW, "prevW"), (foeW, "foeW"))):
                output(x, k, 2 + i, T.U2[:, 256 * i:256 * i + 256], "U2:%d" % i)
            for i, y in ((4, T.yu), (2, T.yp), (3, T.yf)):
                dma("Y", y[:], T.OUT[0:128:16, 256 * i:256 * i + 256], ["out%d" % i], [])
        def names(h):
            p = 512 * t + 256 * h
            mm(XR[h][:, 0:128], T.BOh[:], T.PKl[:, p:p + 128], False, True, ["BOh", "PKl%d%d" % (t, h)], [("q4:X", "q2:X")[h]])
            mm(T.q3[:, half(h, 256)], T.BOh[:], T.PKl[:, p + 128:p + 256], True, True, ["BOh", "PKl%d%d" % (t, h)], ["q3:n%d" % h])
            tt(T.X1[:, half(h)], XR[h][:, 0:128], T.OD[:, half(h)], A.max, [("q4:X", "q2:X")[h], "OD"], ["X1%d" % h])
            ts(T.O[:, half(h)], T.X1[:, half(h)], W - 1, None, A.bitwise_and, None, ["X1%d" % h], ["O%d" % h])

        def new_targets(h):
            tt(T.SM[:, half(h)], T.q3[:, half(h, 256)], T.MW[:, half(h)], A.mult, ["q3:n%d" % h, "MW"], ["SM"])
            scan(T.EXp[:, half(h)], T.RST[:, half(h)], T.SM[:, half(h)], A.mult, A.add, ["RST", "SM"], ["EXp"])
            if h == 1:
                tt(nbm, T.EXp[:, 15:256:16], mth, A.mult, ["EXp", "mth"], ["nbm"])
                tt(tauW, nbm, base2, A.add, ["nbm", "base2"], ["tauW"])

        if not last:
            names(0)
            home_look(0)
            home_gather(t + 1, 0)
            new_targets(0)
            home_gather(t + 1, 1)
            names(1)
            new_targets(1)
            send_targets(t + 1)
            home_look(1)
            home_gather(t + 1, 2)
            own_place(prevW, "prevW", T.Xps[:, s1], "Xps%d" % (t + 1))
            send_prevs(t + 1)
        else:
            for h in (0, 1):
                names(h)
                new_targets(h)
                cp(T.OUT[:, half(h)], T.O[:, half(h)], ["O%d" % h], ["out0"])
            dma("Y", T.yo[:], T.OUT[:, 0:256], ["out0"], [])
            output(tauW, "tauW", 1, T.U2[:, 0:256], "U2:0")
            dma("S", T.yt[:], T.OUT[0:128:16, 256:512], ["out1"], [])

    for i in plan(prog):
        issue(*prog[i][:5])
    for k in sorted(cnt):
        if cnt[k]:
            need("G", k, cnt[k])
    for k in range(ndma[0]):
        need("G", "d%d" % k, 16)
    for x in sorted(wr):
        if wr[x][0][0] == "a":
            need("G", *wr[x])
